import numpy as np, ml_dtypes
CORES = [9,25,41,57]
N = 4
import mx_ref
BF = ml_dtypes.bfloat16
def entries(a):
    return np.ascontiguousarray(a.T).reshape(-1)
def table(e):
    return np.ascontiguousarray(np.reshape(e, (-1, 16)).T).astype(np.int32)
def pick(q, e):
    c = np.concatenate([q[0].reshape(128, -1, 4), np.zeros((128, 1, 4), np.uint8)], axis=1); s = np.concatenate([q[1], np.ones((16, 1), np.uint8)], axis=1)
    return (np.ascontiguousarray(c[:, e].reshape(128, -1)), np.ascontiguousarray(s[:, e]))
def join(*qs):
    return (np.concatenate([q[0] for q in qs], axis=1), np.concatenate([q[1] for q in qs], axis=1))
def put(q, e, v):
    c, s = q[0].reshape(128, -1, 4).copy(), q[1].copy(); c[:, e] = v[0].reshape(128, -1, 4); s[:, e] = v[1]
    return (c.reshape(128, -1), s)
def pk(c, s):
    return (np.ascontiguousarray(c), mx_ref.live(s))
def emit(q):
    return q[0], q[1]
def packed(v, rng):
    q = [mx_ref.quantize(np.ascontiguousarray(v[r])) for r in range(N)]
    return np.stack([a for a, b in q]), np.stack([mx_ref.plane(b, rng) for a, b in q])
def cols(t, e):
    v = np.concatenate([t.reshape(128, -1, 4), np.zeros((128, 1, 4), BF)], axis=1)
    return np.ascontiguousarray(v[:, e]).reshape(128, -1)
def f(rng, *shape):
    return mx_ref.flush((rng.standard_normal(shape, dtype=np.float32) * np.exp2(rng.integers(-2, 3, shape[:-1] + (1,)))).astype(BF))
def wide(rng, *shape, cols=0):
    v = rng.standard_normal(shape, dtype=np.float32) * np.exp2(rng.integers(-12, 13, shape)).astype(np.float32)
    if cols: v *= np.repeat(np.exp2(rng.integers(-cols, cols + 1, shape[:-2] + (1, shape[-1] // 4))) * (rng.random(shape[:-2] + (1, shape[-1] // 4)) > 0.0625), 4, axis=-1).astype(np.float32)
    return mx_ref.flush(v.astype(BF))
T, C, CAPP, M = 512, 1024, 96, 256
def first(v):
    z = np.zeros((N, 128, 512), BF); z[:, :, :4] = v; return z
def lists(rng, full=False, one=False, odd=False):
    h = int(rng.integers(0, N)); a = rng.permutation(np.delete(np.arange(N), h))
    sn = np.full((N, N, CAPP), -1)
    for d in range(N):
        m, o = int(rng.integers(1, M + 1)), rng.permutation(N * CAPP)
        if odd: m = 2 * int(rng.integers(0, M // 2)) + 1
        if full:
            w = np.isin(o // CAPP, a[:M // CAPP] if d == h else a[:1]); o = np.concatenate([o[w], o[~w]])
            m = M if d == h else int(rng.integers(CAPP, M + 1))
        if one: o = o[o // CAPP != a[0]]
        if one and d == h: m, o = 1, o[o // CAPP != h]
        o = o[:m]
        sn[o // CAPP, d, o % CAPP] = rng.integers(0, T, m)
    return np.stack([table(sn[s]) for s in range(N)])
def setup_inputs(rng):
    kc, ks = packed(f(rng, N, 128, 4 * C), rng)
    return {"x": f(rng, N, 128, 4 * T), "u": first(f(rng, N, 128, 4)), "w": f(rng, N, 128, 512), "kc": kc, "ks": ks, "sn": lists(rng)}
def setup_inputs_full(rng):
    return {**setup_inputs(rng), "sn": lists(rng, full=True)}
def setup_inputs_high(rng):
    d = setup_inputs(rng); g = np.where(rng.permutation(N) < N // 2, 1, -1).astype(np.float32)[:, None, None]
    p = rng.permutation(N)
    g = g * np.where(p < N // 2, 2.0 ** 24, 2.0 ** -24).astype(np.float32)[:, None, None]
    k = np.where(p == N - 1, 2.0 ** -24, 2.0 ** 24).astype(np.float32)[:, None, None]
    d["u"] = first(((np.abs(f(rng, N, 128, 4).astype(np.float32)) + 1) * k).astype(BF))
    d["kc"], d["ks"] = packed((g * (1 + np.abs(f(rng, N, 128, 4 * C).astype(np.float32)))).astype(BF), rng); return d
def setup_inputs_one(rng):
    return {**setup_inputs(rng), "sn": lists(rng, one=True)}
def setup_inputs_spread(rng):
    d = setup_inputs(rng); d["x"] = wide(rng, N, 128, 4 * T, cols=8)
    d["kc"], d["ks"] = packed(wide(rng, N, 128, 4 * C, cols=8), rng); return d
def setup_inputs_ties(rng):
    d = setup_inputs(rng); v = f(rng, N, 128, C // 8 * 4)
    d["kc"], d["ks"] = packed(np.stack([cols(v[r], rng.permutation(np.arange(C) // 8)) for r in range(N)]), rng)
    d["u"][int(rng.integers(0, N))] = 0
    d["sn"] = lists(rng, odd=True); return d
def scores(u, kc, ks):
    return mx_ref.matmul(mx_ref.quantize(np.ascontiguousarray(u)), pk(kc, ks))[0] + np.float32(0)
def check_inputs(d):
    b = []
    for r in range(N):
        if (d["u"][r][:, 4:].astype(np.float32) != 0).any(): b.append("u")
        e = entries(d["sn"][r])
        m = sum(int((entries(d["sn"][s])[r * CAPP:r * CAPP + CAPP] >= 0).sum()) for s in range(N))
        if e.min() < -1 or e.max() >= T or m < 1 or m > M: b.append("sn")
        try: good = bool(np.isfinite(scores(d["u"][r], d["kc"][r], d["ks"][r])).all())
        except Exception: good = False
        if not good: b.append("kc")
    return b
def reference(x, u, w, kc, ks, sn):
    oc, osc, ev = np.zeros((N, 128, 4 * C), np.uint8), np.zeros((N, 16, C), np.uint8), np.zeros((N, 2, M), np.float32)
    y = np.zeros((N, 128, C), np.float32)
    new = join(*[mx_ref.quantize(np.ascontiguousarray(x[s])) for s in range(N)])
    for d in range(N):
        e = []
        for s in range(N):
            v = entries(sn[s])[d * CAPP:d * CAPP + CAPP]; e.append(s * T + v[v >= 0])
        e = np.concatenate(e); m = e.size
        z = scores(u[d], kc[d], ks[d])
        out = np.argsort(z, kind="stable")[:m]
        after = put(pk(kc[d], ks[d]), out, pick(new, e))
        oc[d], osc[d] = emit(after)
        ev[d, 0] = -1; ev[d, 0, :m] = out; ev[d, 1, :m] = z[out]
        y[d] = mx_ref.matmul(mx_ref.quantize(np.ascontiguousarray(w[d])), after)
    return {"oc": oc, "osc": osc, "ev": ev, "y": y}

@@ -1,0 +1,268 @@
+from concourse.bass import DstId, RemoteDMATransfer
+from concourse.mybir import dt, AluOpType as ALU, ActivationFunctionType as ACT
+
+NR, NT, NC, CAP, MX = 4, 512, 1024, 96, 256
+NW = NC + NR * CAP
+LC = CAP // 16
+BLK = [0, 4, 1, 5, 2, 6, 3, 7]
+NSB = 3
+TINY = 2.0 ** -120
+NP, PW = 4, 256
+
+SCRATCH = {"psv": ("psum", [128, 1024], "float32"), "pss": ("psum", [128, 1024], "float32"), "py": ("psum", [128, 2048], "float32")}
+_SPEC = {
+    "float8_e4m3fn_x4": "uq 272 xq 512 wq 128 sndq 384 winq 1408 aftq 1024",
+    "uint8": "us 272 xs 512 wsc 128 snds 384 wins 1408 afts 1024",
+    "int32": "sn8 24 ll 24 pi 8 pa 8 vo0 8 kk0 32 kk1 32",
+    "uint16": "su 24 lu 24 rkd 16 rkn 8 off 64 vo 8 pm 4",
+    "bfloat16": "u0 4 ua 1088 xt 2048 wt 512 eq 1024 eqm 1024 w01 528 csg 768 cm3 1024 cm4 1024 cm5 1024 cm6 1024 cm7 1024 sg0 1024 sg1 1024 sg2 1024",
+    "float16": "co 512 scn 2560",
+    "float32": "df0 1024 df1 1024 df2 1024 scol 8 nscol 8 acc1 8 acc2 8 ub 8 ub2 8 ub3 8 cnt 8 fl 384 incl 384 csum 2 ksl 2 kfl 2 a2 64 b2 64 "
+               "pos 1024 pt 256 it 64 tt 64 tm 64 ysb 1024 pf 8 kcol 2 kcoh 2 jp0 64 jp 64 vj0 128 vj 128 vs 128 pm0 4 kk 32 "
+               "sr 1024 ej 1024 es 1024 tj 256 ts 256 ex 16 er 64 e0 32 e1 32 e2 32 e3 32 e4 32 em 32 eg 32",
+}
+for _d in _SPEC:
+    _w = _SPEC[_d].split()
+    for _i in range(0, len(_w), 2):
+        SCRATCH[_w[_i]] = ("sbuf", [128, int(_w[_i + 1])], _d)
+SEMAPHORES = "qv qs qt qg lsn lu0 lk0 lk1 lks lx lw lown own hop evx sto larr carr sent".split()
+
+
+def rank_program(g, core, T, topo):
+    me = T.rank_of(core)
+    if me is None:
+        return
+    seen, total = {}, {}
+    v, queues = g.vector, {"v": g.vector, "s": g.scalar, "t": g.tensor, "g": g, "y": g.sync}
+    u8, u32, FL = dt.uint8, dt.uint32, {"allow_small_or_imprecise_dtypes": True}
+
+    def wait(q, deps):
+        for name, val in deps:
+            if seen.get((q, name), 0) < val:
+                queues[q].wait_ge(T.sem[name], val)
+                seen[(q, name)] = val
+
+    def tick(name, n):
+        total[name] = total.get(name, 0) + n
+        return (name, total[name])
+
+    def V(deps, f, *a):
+        wait("v", deps); f(*a).then_inc(T.sem.qv, 1); return tick("qv", 1)
+
+    def S(deps, out, in_, func, **k):
+        wait("s", deps); g.scalar.activation(out, in_, func, **k).then_inc(T.sem.qs, 1); return tick("qs", 1)
+
+    def P(deps, *a):
+        wait("t", deps); g.tensor.matmul_mx(*a).then_inc(T.sem.qt, 1); return tick("qt", 1)
+
+    def G(deps, f, *a, **k):
+        wait("g", list(deps) + [("qg", total.get("qg", 0))]); f(*a, **k).then_inc(T.sem.qg, 1); return tick("qg", 1)
+
+    def D(q, deps, sem, out, in_):
+        wait(q, deps); queues[q].dma_start(out, in_).then_inc(T.sem[sem], 16); return tick(sem, 16)
+
+    k0 = D("y", [], "lk0", T.winq[:, 0:512].bitcast(u8), T.kc[:, 0:2048])
+    k1 = D("y", [], "lk1", T.winq[:, 512:1024].bitcast(u8), T.kc[:, 2048:4096])
+    xl = D("y", [], "lx", T.xt[:], T.x[:])
+    wl = D("y", [], "lw", T.wt[:], T.w[:])
+    u0 = D("s", [], "lu0", T.u0[:], T.u[:, 0:4])
+    ks = D("s", [], "lks", T.wins[:, 0:1024], T.ks[:])
+    for q in range(8):
+        sn = D("s", [], "lsn", T.sn8[16 * q:16 * q + 16, :], T.sn[:])
+
+    c_p = G([], g.iota, T.pi[:, 0:1], [[0, 1]], 0, 1)
+    c_vo = G([], g.iota, T.vo0[:], [[128, 4], [512, 2]], 0, 1)
+    for a in range(4):
+        c_k = G([], g.iota, T.kcol[32 * a:32 * a + 32, :], [[32, 2]], 64 * a, 1, **FL)
+    c_pm = G([], g.iota, T.pm0[:], [[32, 2], [2, 2]], 0, 0, **FL)
+
+    others = [d for d in range(NR) if d != me]
+    emask = {d: sum(1 << e for e in topo.engines(core, T.cores[d])[2 * i:2 * i + 2]) for i, d in enumerate(others)}
+
+    def send(deps, sem, src, dst):
+        wait("g", deps)
+        tr = []
+        for d in others:
+            rid, pid = topo.addr(T.cores[d])[0:2]
+            tr.append(RemoteDMATransfer(dst_ids=[DstId(rid=rid, pnc=pid)], dma_engine_mask=emask[d], remote_sem=T.sem[sem],
+                                        src=src(d), dst=dst(d)))
+        g.remote_dma_fused(tr, local_sem=T.sem.sent)
+        tick("sent", 2 * len(others))
+
+    send([sn], "larr", lambda d: T.sn8[:, LC * d:LC * d + LC], lambda d: T.ll[:, LC * me:LC * me + LC])
+    larr = tick("larr", 2 * len(others))
+    lown = D("y", [sn], "lown", T.ll[:, LC * me:LC * me + LC], T.sn8[:, LC * me:LC * me + LC])
+    c_kk = G([], g.iota, T.kk0[0:16, :], [[1, 32]], 0, 32)
+    c_jp = G([], g.iota, T.jp0[:], [[512, 2], [16, 8], [128, 4]], 0, 0, **FL)
+    c_vj = G([], g.iota, T.vj0[:], [[128, 4], [512, 2], [1, 16]], 0, 0, **FL)
+
+    z_u = V([], v.memset, T.ua[:, 512:1088], 0.0)
+    V([c_p], v.tensor_scalar, T.pa[:, 0:1], T.pi[:, 0:1], 15, None, ALU.bitwise_and)
+    V([], v.tensor_scalar, T.pa[:, 1:2], T.pi[:, 0:1], 112, None, ALU.bitwise_and)
+    V([], v.tensor_scalar, T.pa[:, 2:3], T.pi[:, 0:1], 7, None, ALU.bitwise_and)
+    a4 = V([], v.tensor_scalar, T.pa[:, 3:4], T.pi[:, 0:1], 3, 1, ALU.logical_shift_right, ALU.bitwise_and)
+    z1 = V([], v.memset, T.w01[:], 1.0)
+    f4 = V([a4], v.tensor_copy, T.pf[:, 0:4], T.pa[:, 0:4])
+    z2 = V([z1], v.memset, T.w01[:, 0:1], 0.0)
+    f7 = V([], v.tensor_scalar, T.pf[:, 6:7], T.pi[:, 0:1], 8, None, ALU.is_lt)
+    f5 = V([f4], v.tensor_scalar, T.pf[:, 4:5], T.pf[:, 2:3], 4.0, None, ALU.mult)
+    vo = V([c_vo], v.tensor_copy, T.vo[:], T.vo0[:])
+    f6 = V([f5], v.tensor_tensor, T.pf[:, 5:6], T.pf[:, 4:5], T.pf[:, 3:4], ALU.add)
+    kc = V([c_k], v.tensor_scalar, T.kcoh[:], T.kcol[:], 0.5, None, ALU.add)
+    pm = V([f6, c_pm], v.tensor_scalar, T.pm[:], T.pm0[:], T.pf[:, 5:6], None, ALU.add)
+    t = V([u0], v.tensor_copy, T.ua[:, 0:4], T.u0[:])
+    V([z_u], v.tensor_copy, T.ua[:, 4 * 142:4 * 143], T.u0[:])
+    n = 4
+    while n < 512:
+        t = V([t], v.tensor_copy, T.ua[:, n:2 * n], T.ua[:, 0:n])
+        n *= 2
+    uq = V([t], v.quantize_mx, T.uq[:], T.us[:], T.ua[:])
+    su = V([sn], v.tensor_copy, T.su[:], T.sn8[:])
+    z3 = V([], v.memset, T.a2[:], 0.0)
+    z4 = V([], v.memset, T.acc1[:], 0.0)
+    z5 = V([], v.memset, T.e1[0:32, :], 0.0)
+    kk1 = V([c_kk], v.tensor_scalar, T.kk1[0:16, :], T.kk0[0:16, :], MX - 1, None, ALU.bitwise_and)
+    jp = V([c_jp], v.tensor_scalar, T.jp[:], T.jp0[:], T.pf[:, 0:1], None, ALU.add)
+    kk = V([kk1], v.tensor_copy, T.kk[0:16, :], T.kk1[0:16, :])
+    vj = V([c_vj], v.tensor_scalar, T.vj[:], T.vj0[:], T.pf[:, 1:2], None, ALU.add)
+    z6 = V([], v.memset, T.ej[:, 0:MX], 0.0)
+    z7 = V([], v.memset, T.es[:, 0:MX], 0.0)
+    z8 = V([], v.memset, T.pos[:, MX:NC], 0.0)
+
+    def row(ps, h, deps):
+        a, b = 512 * h, 512 * h + 512
+        return P(deps, ps[:, a:b], T.uq[:, 0:128], T.us[:, 0:128], T.winq[:, a:b], T.wins[:, a:b], True, True)
+
+    def col(i, start, stop, deps):
+        b, o = 128 * BLK[i], 142 - 2 * i
+        return P(deps, T.py[:, 0:128], T.winq[:, b:b + 128], T.wins[:, b:b + 128], T.uq[:, o:o + 128], T.us[:, o:o + 128], start, stop)
+
+    row(T.psv, 0, [uq, ks, k0])
+    row(T.pss, 0, [])
+    for n, i in enumerate((0, 2, 4, 6)):
+        col(i, n == 0, False, [])
+    for n, i in enumerate((1, 3, 5, 7)):
+        cols = col(i, False, n == 3, [k1])
+    rv = row(T.psv, 1, [])
+    rs = row(T.pss, 1, [])
+
+    nsc = V([cols], v.tensor_scalar, T.nscol[:], T.py[:, 0:16:2], -1.0, None, ALU.mult)
+    sc = V([cols], v.tensor_copy, T.scol[:], T.py[:, 0:16:2])
+
+    def s_diff(i):
+        return S([rs, nsc], T["df%d" % i][:], T.pss[:], ACT.Identity, bias=T.nscol[:, i:i + 1])
+
+    def s_sign(i, d):
+        b, df, sg = 128 * BLK[i], T["df%d" % i], T["sg%d" % i]
+        if b:
+            S([d, z4], sg[:, 0:b], df[:, 0:b], ACT.Sign, bias=TINY, scale=-1.0, accum_out=T.acc1[:, i:i + 1])
+        return S([d], sg[:, b:1024], df[:, b:1024], ACT.Sign, bias=-TINY, scale=-1.0, accum_out=T.acc2[:, i:i + 1])
+
+    def v_cmp(i):
+        b, cm = 128 * BLK[i], T["cm%d" % i]
+        V([rv, sc], v.tensor_scalar, cm[:, 0:b], T.psv[:, 0:b], T.scol[:, i:i + 1], None, ALU.is_le)
+        return V([], v.tensor_scalar, cm[:, b:1024], T.psv[:, b:1024], T.scol[:, i:i + 1], None, ALU.is_lt)
+
+    def v_sum(i, c):
+        cm, o = T["cm%d" % i], 512 * (i - NSB)
+        return V([c], v.tensor_tensor_scan, T.scn[:, o:o + 512], cm[:, 0:512], cm[:, 512:1024], 0.0, ALU.add, ALU.add)
+
+    for i in range(8):
+        b = 128 * BLK[i]
+        eq = V([sc, rv], v.tensor_scalar, T.eq[:, 128 * i:128 * i + 128], T.psv[:, b:b + 128], T.scol[:, i:i + 1], None, ALU.is_equal)
+    eqm = G([eq], g.affine_select, T.eqm[:], T.eq[:], [[0, 8], [-1, 128]], ALU.is_gt, 0.0, 0, 1)
+
+    d0 = s_diff(0)
+    c3 = v_cmp(3)
+    xq = V([xl], v.quantize_mx, T.xq[:], T.xs[:], T.xt[:])
+    c4 = v_cmp(4)
+    s_sign(0, d0)
+    pq = V([xq, su], v.tensor_copy, T.sndq[:].bitcast(u32), T.xq[:].bitcast(u32).indirect(T.su[:]))
+    ps = S([xq, su], T.snds[:], T.xs[:].indirect(T.su[:]), ACT.Copy)
+    w0, own0 = NC + CAP * me, CAP * me
+    send([pq], "carr", lambda d: T.sndq[:, CAP * d:CAP * d + CAP].bitcast(u8), lambda d: T.winq[:, w0:w0 + CAP].bitcast(u8))
+    send([ps], "carr", lambda d: T.snds[:, CAP * d:CAP * d + CAP], lambda d: T.wins[:, w0:w0 + CAP])
+    carr = tick("carr", 4 * len(others))
+    D("y", [pq], "own", T.winq[:, w0:w0 + CAP].bitcast(u8), T.sndq[:, own0:own0 + CAP].bitcast(u8))
+    own = D("y", [ps], "own", T.wins[:, w0:w0 + CAP], T.snds[:, own0:own0 + CAP])
+
+    v_sum(3, c3)
+    lu = V([larr, lown], v.tensor_scalar, T.lu[:], T.ll[:], 1.0, None, ALU.add)
+    d1 = s_diff(1)
+    fl = S([lu, z2], T.fl[:], T.w01[:].indirect(T.lu[:]), ACT.Copy)
+    s_sign(1, d1)
+    c5 = v_cmp(5)
+    incl = V([fl], v.tensor_tensor_scan, T.incl[:], T.fl[:], T.fl[:], 0.0, ALU.add, ALU.max)
+    v_sum(4, c4)
+    for h in range(2):
+        cs = S([incl, kc], T.csg[:, 384 * h:384 * h + 384], T.incl[:], ACT.Sign, bias=T.kcoh[:, h:h + 1], scale=-1.0, accum_out=T.csum[:, h:h + 1])
+    d2 = s_diff(2)
+    sg = s_sign(2, d2)
+    c6 = v_cmp(6)
+    v_sum(5, c5)
+    for i in range(8):
+        a = 128 * i
+        co = V([eqm], v.tensor_tensor_scan, T.co[:, 64 * i:64 * i + 64], T.eqm[:, a:a + 64], T.eqm[:, a + 64:a + 128], 0.0, ALU.add, ALU.add)
+    sl = V([cs], v.tensor_scalar, T.ksl[:], T.csum[:], 0.5, float(NC + NR * CAP // 2), ALU.mult, ALU.add)
+    c7 = v_cmp(7)
+    kf = V([sl], v.tensor_scalar, T.kfl[:], T.ksl[:], float(NW), None, ALU.is_lt)
+    v_sum(6, c6)
+    km = V([kf, z3], v.tensor_tensor, T.a2[:, 0:64:32], T.ksl[:], T.kfl[:], ALU.mult)
+    ub = V([co], v.tensor_scalar, T.ub[:, 0:NSB], T.co[:, 63:64 * NSB:64], 2.0, 1024.0, ALU.mult, ALU.add)
+    em = V([kk, incl], v.tensor_scalar, T.em[0:16, :], T.kk[0:16, :], T.incl[0:16, NR * CAP - 1:NR * CAP], None, ALU.is_lt)
+    b2 = V([km], v.transpose, T.b2[:], T.a2[:])
+    for a in range(4):
+        pos = G([b2], g.partition_broadcast, T.pos[:, 64 * a:64 * a + 64], T.b2[32 * a:32 * a + 1, :], 128)
+    sm = v_sum(7, c7)
+    eg = V([em, f7], v.tensor_scalar, T.eg[0:16, :], T.em[0:16, :], -1.0, T.pf[0:16, 6:7], ALU.add, ALU.mult)
+    wq = V([wl], v.quantize_mx, T.wq[:], T.wsc[:], T.wt[:])
+
+    ub2 = V([ub, sg], v.tensor_tensor, T.ub2[:, 0:NSB], T.ub[:, 0:NSB], T.acc1[:, 0:NSB], ALU.add)
+    V([sm], v.tensor_tensor, T.cnt[:, NSB:8], T.scn[:, 511:512 * (8 - NSB):512], T.co[:, 64 * NSB + 63:512:64], ALU.add)
+    ub3 = V([ub2], v.tensor_tensor, T.ub3[:, 0:NSB], T.ub2[:, 0:NSB], T.acc2[:, 0:NSB], ALU.add)
+    cn = V([ub3], v.tensor_scalar, T.cnt[:, 0:NSB], T.ub3[:, 0:NSB], 0.5, None, ALU.mult)
+    V([cn], v.tensor_copy, T.rkd[:, 0:16:2], T.cnt[:])
+    rd = V([], v.tensor_copy, T.rkd[:, 1:16:2], T.cnt[:])
+    pt = V([rd, pos, z8], v.tensor_copy, T.pt[:], T.pos[:].indirect(T.rkd[:]))
+    for a in range(4):
+        hop = D("y", [pt], "hop", T.it[32 * a:32 * a + 32, :], T.pt[a:128:16, :])
+
+    sr = S([], T.sr[:], T.pss[:], ACT.Copy)
+    vs = S([sr, vo], T.vs[:], T.sr[:].indirect(T.vo[:]), ACT.Copy)
+    rn = V([], v.tensor_copy, T.rkn[:], T.cnt[:])
+    ej = V([rn, z6, vj], v.tensor_copy, T.ej[:].indirect(T.rkn[:]), T.vj[:])
+    es = V([vs, z7], v.tensor_copy, T.es[:].indirect(T.rkn[:]), T.vs[:])
+    tj = V([ej], v.transpose, T.tj[:], T.ej[:, 0:MX])
+    ts = V([es], v.transpose, T.ts[:], T.es[:, 0:MX])
+    V([tj], v.tensor_tensor, T.ex[:, 0:8], T.tj[:, 0:MX:32], T.tj[:, 16:MX:32], ALU.add)
+    ex = V([ts], v.tensor_tensor, T.ex[:, 8:16], T.ts[:, 0:MX:32], T.ts[:, 16:MX:32], ALU.add)
+    for a in range(4):
+        evx = D("y", [ex], "evx", T.er[0:32, 16 * a:16 * a + 16], T.ex[32 * a:32 * a + 32, :])
+
+    tt = V([hop], v.transpose, T.tt[:], T.it[:])
+    tm = V([tt, jp], v.tensor_tensor, T.tm[:], T.tt[:], T.jp[:], ALU.max)
+    off = V([tm, pm], v.tensor_copy, T.off[:], T.tm[:].indirect(T.pm[:]))
+
+    pl, mm = [], []
+    for i in range(NP):
+        a, b, o = PW * i, PW * i + PW, T.off[:, PW // 16 * i:PW // 16 * (i + 1)]
+        pc = V([off, k0, k1, own, carr], v.tensor_copy, T.aftq[:, a:b].bitcast(u32), T.winq[:].bitcast(u32).indirect(o))
+        pl = S([off, ks, own, carr], T.afts[:, a:b], T.wins[:].indirect(o), ACT.Copy)
+        mm.append(P([pc, pl, wq, sc], T.py[:, 512 * i:512 * i + PW], T.wq[:], T.wsc[:], T.aftq[:, a:b], T.afts[:, a:b], True, True))
+        D("y", [pc], "sto", T.oc[:, 4 * a:4 * b], T.aftq[:, a:b].bitcast(u8))
+    e0 = V([evx], v.tensor_tensor, T.e0[0:32, :], T.er[0:32, 0:32], T.er[0:32, 32:64], ALU.add)
+    e1 = V([e0, z5], v.tensor_tensor, T.e1[0:32, 0:16], T.e0[0:32, 0:16], T.e0[0:32, 16:32], ALU.add)
+    e2 = V([e1], v.transpose, T.e2[0:32, :], T.e1[0:32, :])
+    e3 = V([e2, em], v.tensor_tensor, T.e3[0:16, :], T.e2[0:16, :], T.em[0:16, :], ALU.mult)
+    e4 = V([e3, eg], v.tensor_tensor, T.e4[0:16, :], T.e3[0:16, :], T.eg[0:16, :], ALU.add)
+    for i in range(NP):
+        o, p = T.ysb[:, PW * i:PW * i + PW], T.py[:, 512 * i:512 * i + PW]
+        yc = S([mm[i]], o, p, ACT.Copy) if i < NP - 1 else V([mm[i]], v.tensor_copy, o, p)
+        D("y", [yc], "sto", T.y[:, PW * i:PW * i + PW], o)
+    for k in range(4):
+        D("s", [pl], "sto", T.osc[4 * k:4 * k + 4, :], T.afts[32 * k:32 * k + 4, :])
+    D("s", [e4], "sto", T.ev[:], T.e4[0:16, :])
+
+    for name in SEMAPHORES:
+        if name in total:
+            wait("g", [(name, total[name])])

@@ -5,7 +5,6 @@ NR, NT, NC, CAP, MX = 4, 512, 1024, 96, 256
 NW = NC + NR * CAP
 LC = CAP // 16
 BLK = [0, 4, 1, 5, 2, 6, 3, 7]
-NSB = 3
 TINY = 2.0 ** -120
 NP, PW = 4, 256
 
@@ -13,19 +12,19 @@ SCRATCH = {"psv": ("psum", [128, 1024], "float32"), "pss": ("psum", [128, 1024],
 _SPEC = {
     "float8_e4m3fn_x4": "uq 272 xq 512 wq 128 sndq 384 winq 1408 aftq 1024",
     "uint8": "us 272 xs 512 wsc 128 snds 384 wins 1408 afts 1024",
-    "int32": "sn8 24 ll 24 pi 8 pa 8 vo0 8 kk0 32 kk1 32",
-    "uint16": "su 24 lu 24 rkd 16 rkn 8 off 64 vo 8 pm 4",
-    "bfloat16": "u0 4 ua 1088 xt 2048 wt 512 eq 1024 eqm 1024 w01 528 csg 768 cm3 1024 cm4 1024 cm5 1024 cm6 1024 cm7 1024 sg0 1024 sg1 1024 sg2 1024",
+    "int32": "sn8 24 ll 24 pi 8 pa 16 vo0 8 kk0 32 kk1 32",
+    "uint16": "su 24 lu 24 rkd 16 rkn 8 off 64 vo 8 pm 4 ud 8",
+    "bfloat16": "u0 16 ua 1088 xt 2048 wt 512 eq 1024 eqm 1024 w01 528 csg 768 cm3 512 cm4 1024 cm5 1024 cm6 1024 cm7 1024 sg0 1024 sg1 1024 sg2 1024 sg3 512",
     "float16": "co 512 scn 2560",
-    "float32": "df0 1024 df1 1024 df2 1024 scol 8 nscol 8 acc1 8 acc2 8 ub 8 ub2 8 ub3 8 cnt 8 fl 384 incl 384 csum 2 ksl 2 kfl 2 a2 64 b2 64 "
-               "pos 1024 pt 256 it 64 tt 64 tm 64 ysb 1024 pf 8 kcol 2 kcoh 2 jp0 64 jp 64 vj0 128 vj 128 vs 128 pm0 4 kk 32 "
+    "float32": "df0 1024 df1 1024 df2 1024 df3 512 scol 8 nscol 8 acc1 8 acc2 8 ub 8 ub2 8 ub3 8 cnt 8 fl 384 incl 384 csum 2 ksl 2 kfl 2 a2 64 b2 64 "
+               "pos 1024 pt 256 it 64 tt 64 ysb 1024 pf 8 kcol 2 kcoh 2 js0 256 js 256 vj0 128 vj 128 vs 128 pm0 4 kk 32 "
                "sr 1024 ej 1024 es 1024 tj 256 ts 256 ex 16 er 64 e0 32 e1 32 e2 32 e3 32 e4 32 em 32 eg 32",
 }
 for _d in _SPEC:
     _w = _SPEC[_d].split()
     for _i in range(0, len(_w), 2):
         SCRATCH[_w[_i]] = ("sbuf", [128, int(_w[_i + 1])], _d)
-SEMAPHORES = "qv qs qt qg lsn lu0 lk0 lk1 lks lx lw lown own hop evx sto larr carr sent".split()
+SEMAPHORES = "qv qs qt qg lsn lu0 lk0 lk1 lx lw lown own hop evx sto larr carr sent".split()
 
 
 def rank_program(g, core, T, topo):
@@ -61,20 +60,25 @@ def rank_program(g, core, T, topo):
     def D(q, deps, sem, out, in_):
         wait(q, deps); queues[q].dma_start(out, in_).then_inc(T.sem[sem], 16); return tick(sem, 16)
 
-    k0 = D("y", [], "lk0", T.winq[:, 0:512].bitcast(u8), T.kc[:, 0:2048])
-    k1 = D("y", [], "lk1", T.winq[:, 512:1024].bitcast(u8), T.kc[:, 2048:4096])
+    D("y", [], "lk0", T.winq[:, 0:512].bitcast(u8), T.kc[:, 0:2048])
+    k0 = D("y", [], "lk0", T.wins[:, 0:512], T.ks[:, 0:512])
+    D("y", [], "lk1", T.winq[:, 512:1024].bitcast(u8), T.kc[:, 2048:4096])
+    k1 = D("y", [], "lk1", T.wins[:, 512:1024], T.ks[:, 512:1024])
+    u0 = D("s", [], "lu0", T.u0[:], T.u[:, 0:16])
+    for q in range(8):
+        sn = D("s" if q < 6 else "y", [], "lsn", T.sn8[16 * q:16 * q + 16, :], T.sn[:])
     xl = D("y", [], "lx", T.xt[:], T.x[:])
     wl = D("y", [], "lw", T.wt[:], T.w[:])
-    u0 = D("s", [], "lu0", T.u0[:], T.u[:, 0:4])
-    ks = D("s", [], "lks", T.wins[:, 0:1024], T.ks[:])
-    for q in range(8):
-        sn = D("s", [], "lsn", T.sn8[16 * q:16 * q + 16, :], T.sn[:])
 
-    c_p = G([], g.iota, T.pi[:, 0:1], [[0, 1]], 0, 1)
-    c_vo = G([], g.iota, T.vo0[:], [[128, 4], [512, 2]], 0, 1)
+    c_p = G([], g.iota, T.pi[:], [[0, 8]], 0, 1)
+    c_pm = G([], g.iota, T.pm0[:], [[32, 2], [2, 2]], 0, 0, **FL)
     for a in range(4):
         c_k = G([], g.iota, T.kcol[32 * a:32 * a + 32, :], [[32, 2]], 64 * a, 1, **FL)
-    c_pm = G([], g.iota, T.pm0[:], [[32, 2], [2, 2]], 0, 0, **FL)
+    c_kk = G([], g.iota, T.kk0[0:16, :], [[1, 32]], 0, 32)
+    c_vo = G([], g.iota, T.vo0[:], [[128, 4], [512, 2]], 0, 1)
+    for b in range(4):
+        c_js = G([], g.iota, T.js0[:, 64 * b:64 * b + 64], [[512, 2], [0, 2], [1, 16]], 128 * b, 0, **FL)
+    c_vj = G([], g.iota, T.vj0[:], [[128, 4], [512, 2], [1, 16]], 0, 0, **FL)
 
     others = [d for d in range(NR) if d != me]
     emask = {d: sum(1 << e for e in topo.engines(core, T.cores[d])[2 * i:2 * i + 2]) for i, d in enumerate(others)}
@@ -92,91 +96,94 @@ def rank_program(g, core, T, topo):
     send([sn], "larr", lambda d: T.sn8[:, LC * d:LC * d + LC], lambda d: T.ll[:, LC * me:LC * me + LC])
     larr = tick("larr", 2 * len(others))
     lown = D("y", [sn], "lown", T.ll[:, LC * me:LC * me + LC], T.sn8[:, LC * me:LC * me + LC])
-    c_kk = G([], g.iota, T.kk0[0:16, :], [[1, 32]], 0, 32)
-    c_jp = G([], g.iota, T.jp0[:], [[512, 2], [16, 8], [128, 4]], 0, 0, **FL)
-    c_vj = G([], g.iota, T.vj0[:], [[128, 4], [512, 2], [1, 16]], 0, 0, **FL)
 
     z_u = V([], v.memset, T.ua[:, 512:1088], 0.0)
-    V([c_p], v.tensor_scalar, T.pa[:, 0:1], T.pi[:, 0:1], 15, None, ALU.bitwise_and)
+    a8 = V([c_p], v.tensor_scalar, T.pa[:, 8:16], T.pi[:], 3, None, ALU.bitwise_and)
     V([], v.tensor_scalar, T.pa[:, 1:2], T.pi[:, 0:1], 112, None, ALU.bitwise_and)
+    ud = V([a8], v.tensor_copy, T.ud[:], T.pa[:, 8:16])
     V([], v.tensor_scalar, T.pa[:, 2:3], T.pi[:, 0:1], 7, None, ALU.bitwise_and)
+    V([], v.tensor_scalar, T.pa[:, 0:1], T.pi[:, 0:1], 15, None, ALU.bitwise_and)
     a4 = V([], v.tensor_scalar, T.pa[:, 3:4], T.pi[:, 0:1], 3, 1, ALU.logical_shift_right, ALU.bitwise_and)
-    z1 = V([], v.memset, T.w01[:], 1.0)
-    f4 = V([a4], v.tensor_copy, T.pf[:, 0:4], T.pa[:, 0:4])
-    z2 = V([z1], v.memset, T.w01[:, 0:1], 0.0)
-    f7 = V([], v.tensor_scalar, T.pf[:, 6:7], T.pi[:, 0:1], 8, None, ALU.is_lt)
-    f5 = V([f4], v.tensor_scalar, T.pf[:, 4:5], T.pf[:, 2:3], 4.0, None, ALU.mult)
-    vo = V([c_vo], v.tensor_copy, T.vo[:], T.vo0[:])
-    f6 = V([f5], v.tensor_tensor, T.pf[:, 5:6], T.pf[:, 4:5], T.pf[:, 3:4], ALU.add)
-    kc = V([c_k], v.tensor_scalar, T.kcoh[:], T.kcol[:], 0.5, None, ALU.add)
-    pm = V([f6, c_pm], v.tensor_scalar, T.pm[:], T.pm0[:], T.pf[:, 5:6], None, ALU.add)
-    t = V([u0], v.tensor_copy, T.ua[:, 0:4], T.u0[:])
-    V([z_u], v.tensor_copy, T.ua[:, 4 * 142:4 * 143], T.u0[:])
-    n = 4
-    while n < 512:
-        t = V([t], v.tensor_copy, T.ua[:, n:2 * n], T.ua[:, 0:n])
-        n *= 2
-    uq = V([t], v.quantize_mx, T.uq[:], T.us[:], T.ua[:])
-    su = V([sn], v.tensor_copy, T.su[:], T.sn8[:])
-    z3 = V([], v.memset, T.a2[:], 0.0)
     z4 = V([], v.memset, T.acc1[:], 0.0)
-    z5 = V([], v.memset, T.e1[0:32, :], 0.0)
-    kk1 = V([c_kk], v.tensor_scalar, T.kk1[0:16, :], T.kk0[0:16, :], MX - 1, None, ALU.bitwise_and)
-    jp = V([c_jp], v.tensor_scalar, T.jp[:], T.jp0[:], T.pf[:, 0:1], None, ALU.add)
-    kk = V([kk1], v.tensor_copy, T.kk[0:16, :], T.kk1[0:16, :])
-    vj = V([c_vj], v.tensor_scalar, T.vj[:], T.vj0[:], T.pf[:, 1:2], None, ALU.add)
-    z6 = V([], v.memset, T.ej[:, 0:MX], 0.0)
-    z7 = V([], v.memset, T.es[:, 0:MX], 0.0)
-    z8 = V([], v.memset, T.pos[:, MX:NC], 0.0)
+    z4 = V([], v.memset, T.acc2[:], 0.0)
+    f4 = V([a4], v.tensor_copy, T.pf[:, 0:4], T.pa[:, 0:4])
+    z1 = V([], v.memset, T.w01[:], 1.0)
+    V([u0, z_u], v.tensor_copy, T.ua[:, 4 * 142:4 * 143], T.u0[:, 0:4])
+    t = V([ud], v.tensor_copy, T.ua[:, 0:128], T.u0[:].indirect(T.ud[:]))
+    t = V([t], v.tensor_copy, T.ua[:, 128:256], T.ua[:, 0:128])
+    t = V([t], v.tensor_copy, T.ua[:, 256:512], T.ua[:, 0:256])
+    uq = V([t], v.quantize_mx, T.uq[:], T.us[:], T.ua[:])
+    z2 = V([z1], v.memset, T.w01[:, 0:1], 0.0)
+    f5 = V([f4], v.tensor_scalar, T.pf[:, 4:5], T.pf[:, 2:3], 4.0, None, ALU.mult)
+    kc = V([c_k], v.tensor_scalar, T.kcoh[:], T.kcol[:], 0.5, None, ALU.add)
+    f6 = V([f5], v.tensor_tensor, T.pf[:, 5:6], T.pf[:, 4:5], T.pf[:, 3:4], ALU.add)
+    z3 = V([], v.memset, T.a2[:], 0.0)
+    pm = V([f6, c_pm], v.tensor_scalar, T.pm[:], T.pm0[:], T.pf[:, 5:6], None, ALU.add)
 
-    def row(ps, h, deps):
+    def rows(ps, h):
         a, b = 512 * h, 512 * h + 512
-        return P(deps, ps[:, a:b], T.uq[:, 0:128], T.us[:, 0:128], T.winq[:, a:b], T.wins[:, a:b], True, True)
+        return P([], ps[:, a:b], T.uq[:, 0:128], T.us[:, 0:128], T.winq[:, a:b], T.wins[:, a:b], True, True)
 
-    def col(i, start, stop, deps):
-        b, o = 128 * BLK[i], 142 - 2 * i
-        return P(deps, T.py[:, 0:128], T.winq[:, b:b + 128], T.wins[:, b:b + 128], T.uq[:, o:o + 128], T.us[:, o:o + 128], start, stop)
+    def cols(h, deps):
+        for i in range(h, 8, 2):
+            b, o = 128 * BLK[i], 142 - 2 * i
+            t = P(deps, T.py[:, 512 * h:512 * h + 128], T.winq[:, b:b + 128], T.wins[:, b:b + 128], T.uq[:, o:o + 128], T.us[:, o:o + 128], i == h, i == h + 6)
+        return t
 
-    row(T.psv, 0, [uq, ks, k0])
-    row(T.pss, 0, [])
-    for n, i in enumerate((0, 2, 4, 6)):
-        col(i, n == 0, False, [])
-    for n, i in enumerate((1, 3, 5, 7)):
-        cols = col(i, False, n == 3, [k1])
-    rv = row(T.psv, 1, [])
-    rs = row(T.pss, 1, [])
+    pc = [cols(0, [uq, k0])]
+    rv = [rows(T.psv, 0)]
+    rs = [rows(T.pss, 0)]
+    pc.append(cols(1, [k1]))
+    rv.append(rows(T.psv, 1))
+    rs.append(rows(T.pss, 1))
+    nsc, sc = [], []
 
-    nsc = V([cols], v.tensor_scalar, T.nscol[:], T.py[:, 0:16:2], -1.0, None, ALU.mult)
-    sc = V([cols], v.tensor_copy, T.scol[:], T.py[:, 0:16:2])
+    def columns(h):
+        p = T.py[:, 512 * h + 2 * h:512 * h + 16:4]
+        nsc.append(V([pc[h]], v.tensor_scalar, T.nscol[:, h:8:2], p, -1.0, None, ALU.mult))
+        sc.append(V([pc[h]], v.tensor_copy, T.scol[:, h:8:2], p))
 
-    def s_diff(i):
-        return S([rs, nsc], T["df%d" % i][:], T.pss[:], ACT.Identity, bias=T.nscol[:, i:i + 1])
+    def s_diff(i, a, b):
+        return S([rs[a // 512], rs[(b - 1) // 512], nsc[i % 2]], T["df%d" % i][:, a:b], T.pss[:, a:b], ACT.Identity, bias=T.nscol[:, i:i + 1])
 
-    def s_sign(i, d):
-        b, df, sg = 128 * BLK[i], T["df%d" % i], T["sg%d" % i]
+    def s_sign(i, d, n=NC):
+        b, df, sg, t = min(128 * BLK[i], n), T["df%d" % i], T["sg%d" % i], None
         if b:
-            S([d, z4], sg[:, 0:b], df[:, 0:b], ACT.Sign, bias=TINY, scale=-1.0, accum_out=T.acc1[:, i:i + 1])
-        return S([d], sg[:, b:1024], df[:, b:1024], ACT.Sign, bias=-TINY, scale=-1.0, accum_out=T.acc2[:, i:i + 1])
+            t = S([d, z4], sg[:, 0:b], df[:, 0:b], ACT.Sign, bias=TINY, scale=-1.0, accum_out=T.acc1[:, i:i + 1])
+        if b < n:
+            t = S([d, z4], sg[:, b:n], df[:, b:n], ACT.Sign, bias=-TINY, scale=-1.0, accum_out=T.acc2[:, i:i + 1])
+        return t
 
-    def v_cmp(i):
-        b, cm = 128 * BLK[i], T["cm%d" % i]
-        V([rv, sc], v.tensor_scalar, cm[:, 0:b], T.psv[:, 0:b], T.scol[:, i:i + 1], None, ALU.is_le)
-        return V([], v.tensor_scalar, cm[:, b:1024], T.psv[:, b:1024], T.scol[:, i:i + 1], None, ALU.is_lt)
+    def v_cmp(i, a, b, o=0):
+        m, cm, t = min(max(128 * BLK[i], a), b), T["cm%d" % i], None
+        for lo, hi, op in ((a, m, ALU.is_le), (m, b, ALU.is_lt)):
+            if lo < hi:
+                t = V([rv[lo // 512], rv[(hi - 1) // 512], sc[i % 2]], v.tensor_scalar, cm[:, lo - o:hi - o], T.psv[:, lo:hi], T.scol[:, i:i + 1], None, op)
+        return t
 
-    def v_sum(i, c):
-        cm, o = T["cm%d" % i], 512 * (i - NSB)
-        return V([c], v.tensor_tensor_scan, T.scn[:, o:o + 512], cm[:, 0:512], cm[:, 512:1024], 0.0, ALU.add, ALU.add)
+    def v_sum(i, c, n=NC, init=0.0):
+        cm, o = T["cm%d" % i], 512 * (i - 3)
+        return V([c], v.tensor_tensor_scan, T.scn[:, o + 512 - n // 2:o + 512], cm[:, 0:n // 2], cm[:, n // 2:n], init, ALU.add, ALU.add)
 
-    for i in range(8):
-        b = 128 * BLK[i]
-        eq = V([sc, rv], v.tensor_scalar, T.eq[:, 128 * i:128 * i + 128], T.psv[:, b:b + 128], T.scol[:, i:i + 1], None, ALU.is_equal)
-    eqm = G([eq], g.affine_select, T.eqm[:], T.eq[:], [[0, 8], [-1, 128]], ALU.is_gt, 0.0, 0, 1)
+    def v_eq(h):
+        for i in range(h, 8, 2):
+            b = 128 * BLK[i]
+            t = V([sc[h], rv[h]], v.tensor_scalar, T.eq[:, 128 * i:128 * i + 128], T.psv[:, b:b + 128], T.scol[:, i:i + 1], None, ALU.is_equal)
+        return t
 
-    d0 = s_diff(0)
-    c3 = v_cmp(3)
+    columns(0)
+    s_diff(0, 0, 512)
+    v_eq(0)
+    s_diff(2, 0, 512)
+    v_cmp(4, 0, 512)
+    v_cmp(6, 0, 512)
+    su = V([sn], v.tensor_copy, T.su[:], T.sn8[:])
+    columns(1)
+    eqm = G([v_eq(1)], g.affine_select, T.eqm[:], T.eq[:], [[0, 8], [-1, 128]], ALU.is_gt, 0.0, 0, 1)
+    s_sign(0, s_diff(0, 512, 1024))
+    c4 = v_cmp(4, 512, 1024)
     xq = V([xl], v.quantize_mx, T.xq[:], T.xs[:], T.xt[:])
-    c4 = v_cmp(4)
-    s_sign(0, d0)
+    c6 = v_cmp(6, 512, 1024)
     pq = V([xq, su], v.tensor_copy, T.sndq[:].bitcast(u32), T.xq[:].bitcast(u32).indirect(T.su[:]))
     ps = S([xq, su], T.snds[:], T.xs[:].indirect(T.su[:]), ACT.Copy)
     w0, own0 = NC + CAP * me, CAP * me
@@ -186,81 +193,101 @@ def rank_program(g, core, T, topo):
     D("y", [pq], "own", T.winq[:, w0:w0 + CAP].bitcast(u8), T.sndq[:, own0:own0 + CAP].bitcast(u8))
     own = D("y", [ps], "own", T.wins[:, w0:w0 + CAP], T.snds[:, own0:own0 + CAP])
 
-    v_sum(3, c3)
-    lu = V([larr, lown], v.tensor_scalar, T.lu[:], T.ll[:], 1.0, None, ALU.add)
-    d1 = s_diff(1)
-    fl = S([lu, z2], T.fl[:], T.w01[:].indirect(T.lu[:]), ACT.Copy)
-    s_sign(1, d1)
-    c5 = v_cmp(5)
-    incl = V([fl], v.tensor_tensor_scan, T.incl[:], T.fl[:], T.fl[:], 0.0, ALU.add, ALU.max)
     v_sum(4, c4)
+    d2 = s_diff(2, 512, 1024)
+    z8 = V([], v.memset, T.pos[:, MX:NC], 0.0)
+    lu = V([larr, lown], v.tensor_scalar, T.lu[:], T.ll[:], 1.0, None, ALU.add)
+    fl = S([lu, z2], T.fl[:], T.w01[:].indirect(T.lu[:]), ACT.Copy)
+    s_sign(2, d2)
+    c3 = v_cmp(3, 512, 1024, 512)
+    v_sum(6, c6)
+    incl = V([fl], v.tensor_tensor_scan, T.incl[:], T.fl[:], T.fl[:], 0.0, ALU.add, ALU.max)
+    d1 = s_diff(1, 0, 1024)
+    c5 = v_cmp(5, 0, 1024)
     for h in range(2):
         cs = S([incl, kc], T.csg[:, 384 * h:384 * h + 384], T.incl[:], ACT.Sign, bias=T.kcoh[:, h:h + 1], scale=-1.0, accum_out=T.csum[:, h:h + 1])
-    d2 = s_diff(2)
-    sg = s_sign(2, d2)
-    c6 = v_cmp(6)
-    v_sum(5, c5)
+    s_sign(1, d1)
+    sg = s_sign(3, s_diff(3, 0, 512), 512)
+    v_sum(3, c3, 512, -256.0)
     for i in range(8):
         a = 128 * i
         co = V([eqm], v.tensor_tensor_scan, T.co[:, 64 * i:64 * i + 64], T.eqm[:, a:a + 64], T.eqm[:, a + 64:a + 128], 0.0, ALU.add, ALU.add)
+    js = V([c_js, f4], v.tensor_scalar, T.js[:], T.js0[:], T.pf[:, 1:2], None, ALU.add)
     sl = V([cs], v.tensor_scalar, T.ksl[:], T.csum[:], 0.5, float(NC + NR * CAP // 2), ALU.mult, ALU.add)
-    c7 = v_cmp(7)
+    v_sum(5, c5)
     kf = V([sl], v.tensor_scalar, T.kfl[:], T.ksl[:], float(NW), None, ALU.is_lt)
-    v_sum(6, c6)
+    ub = V([co], v.tensor_scalar, T.ub[:, 0:4], T.co[:, 63:64 * 4:64], 2.0, 1024.0, ALU.mult, ALU.add)
     km = V([kf, z3], v.tensor_tensor, T.a2[:, 0:64:32], T.ksl[:], T.kfl[:], ALU.mult)
-    ub = V([co], v.tensor_scalar, T.ub[:, 0:NSB], T.co[:, 63:64 * NSB:64], 2.0, 1024.0, ALU.mult, ALU.add)
-    em = V([kk, incl], v.tensor_scalar, T.em[0:16, :], T.kk[0:16, :], T.incl[0:16, NR * CAP - 1:NR * CAP], None, ALU.is_lt)
+    V([co], v.tensor_copy, T.cnt[:, 4:8], T.co[:, 64 * 4 + 63:512:64])
     b2 = V([km], v.transpose, T.b2[:], T.a2[:])
     for a in range(4):
         pos = G([b2], g.partition_broadcast, T.pos[:, 64 * a:64 * a + 64], T.b2[32 * a:32 * a + 1, :], 128)
+    c7 = v_cmp(7, 0, 1024)
+    ub2 = V([ub, sg], v.tensor_tensor, T.ub2[:, 0:4], T.ub[:, 0:4], T.acc1[:, 0:4], ALU.add)
     sm = v_sum(7, c7)
-    eg = V([em, f7], v.tensor_scalar, T.eg[0:16, :], T.em[0:16, :], -1.0, T.pf[0:16, 6:7], ALU.add, ALU.mult)
-    wq = V([wl], v.quantize_mx, T.wq[:], T.wsc[:], T.wt[:])
+    ub3 = V([ub2], v.tensor_tensor, T.ub3[:, 0:4], T.ub2[:, 0:4], T.acc2[:, 0:4], ALU.add)
+    cn = V([ub3], v.tensor_scalar, T.cnt[:, 0:4], T.ub3[:, 0:4], 0.5, None, ALU.mult)
 
-    ub2 = V([ub, sg], v.tensor_tensor, T.ub2[:, 0:NSB], T.ub[:, 0:NSB], T.acc1[:, 0:NSB], ALU.add)
-    V([sm], v.tensor_tensor, T.cnt[:, NSB:8], T.scn[:, 511:512 * (8 - NSB):512], T.co[:, 64 * NSB + 63:512:64], ALU.add)
-    ub3 = V([ub2], v.tensor_tensor, T.ub3[:, 0:NSB], T.ub2[:, 0:NSB], T.acc2[:, 0:NSB], ALU.add)
-    cn = V([ub3], v.tensor_scalar, T.cnt[:, 0:NSB], T.ub3[:, 0:NSB], 0.5, None, ALU.mult)
+    cn = V([sm, cn], v.tensor_tensor, T.cnt[:, 3:8], T.scn[:, 511:2560:512], T.cnt[:, 3:8], ALU.add)
     V([cn], v.tensor_copy, T.rkd[:, 0:16:2], T.cnt[:])
     rd = V([], v.tensor_copy, T.rkd[:, 1:16:2], T.cnt[:])
-    pt = V([rd, pos, z8], v.tensor_copy, T.pt[:], T.pos[:].indirect(T.rkd[:]))
+    pt = V([rd, pos, z8, js], v.tensor_tensor, T.pt[:], T.pos[:].indirect(T.rkd[:]), T.js[:], ALU.max)
     for a in range(4):
         hop = D("y", [pt], "hop", T.it[32 * a:32 * a + 32, :], T.pt[a:128:16, :])
 
     sr = S([], T.sr[:], T.pss[:], ACT.Copy)
+    vo = V([c_vo], v.tensor_copy, T.vo[:], T.vo0[:])
     vs = S([sr, vo], T.vs[:], T.sr[:].indirect(T.vo[:]), ACT.Copy)
     rn = V([], v.tensor_copy, T.rkn[:], T.cnt[:])
+    vj = V([c_vj], v.tensor_scalar, T.vj[:], T.vj0[:], T.pf[:, 1:2], None, ALU.add)
+    z6 = V([], v.memset, T.ej[:, 0:MX], 0.0)
+    z7 = V([], v.memset, T.es[:, 0:MX], 0.0)
     ej = V([rn, z6, vj], v.tensor_copy, T.ej[:].indirect(T.rkn[:]), T.vj[:])
+    wq = V([wl], v.quantize_mx, T.wq[:], T.wsc[:], T.wt[:])
     es = V([vs, z7], v.tensor_copy, T.es[:].indirect(T.rkn[:]), T.vs[:])
-    tj = V([ej], v.transpose, T.tj[:], T.ej[:, 0:MX])
-    ts = V([es], v.transpose, T.ts[:], T.es[:, 0:MX])
-    V([tj], v.tensor_tensor, T.ex[:, 0:8], T.tj[:, 0:MX:32], T.tj[:, 16:MX:32], ALU.add)
-    ex = V([ts], v.tensor_tensor, T.ex[:, 8:16], T.ts[:, 0:MX:32], T.ts[:, 16:MX:32], ALU.add)
-    for a in range(4):
-        evx = D("y", [ex], "evx", T.er[0:32, 16 * a:16 * a + 16], T.ex[32 * a:32 * a + 32, :])
 
     tt = V([hop], v.transpose, T.tt[:], T.it[:])
-    tm = V([tt, jp], v.tensor_tensor, T.tm[:], T.tt[:], T.jp[:], ALU.max)
-    off = V([tm, pm], v.tensor_copy, T.off[:], T.tm[:].indirect(T.pm[:]))
+    off = V([tt, pm], v.tensor_copy, T.off[:], T.tt[:].indirect(T.pm[:]))
 
-    pl, mm = [], []
+    mm = []
     for i in range(NP):
         a, b, o = PW * i, PW * i + PW, T.off[:, PW // 16 * i:PW // 16 * (i + 1)]
-        pc = V([off, k0, k1, own, carr], v.tensor_copy, T.aftq[:, a:b].bitcast(u32), T.winq[:].bitcast(u32).indirect(o))
-        pl = S([off, ks, own, carr], T.afts[:, a:b], T.wins[:].indirect(o), ACT.Copy)
-        mm.append(P([pc, pl, wq, sc], T.py[:, 512 * i:512 * i + PW], T.wq[:], T.wsc[:], T.aftq[:, a:b], T.afts[:, a:b], True, True))
-        D("y", [pc], "sto", T.oc[:, 4 * a:4 * b], T.aftq[:, a:b].bitcast(u8))
+        t = V([off, k0, k1, own, carr], v.tensor_copy, T.aftq[:, a:b].bitcast(u32), T.winq[:].bitcast(u32).indirect(o))
+        pl = S([off, k0, k1, own, carr], T.afts[:, a:b], T.wins[:].indirect(o), ACT.Copy)
+        mm.append(P([t, pl, wq, sc[1]], T.py[:, 512 * i:512 * i + PW], T.wq[:], T.wsc[:], T.aftq[:, a:b], T.afts[:, a:b], True, True))
+        D("y", [t], "sto", T.oc[:, 4 * a:4 * b], T.aftq[:, a:b].bitcast(u8))
+        if i == 0:
+            tj = V([ej], v.transpose, T.tj[:], T.ej[:, 0:MX])
+            ts = V([es], v.transpose, T.ts[:], T.es[:, 0:MX])
+        if i == 1:
+            V([tj], v.tensor_tensor, T.ex[:, 0:8], T.tj[:, 0:MX:32], T.tj[:, 16:MX:32], ALU.add)
+            ex = V([ts], v.tensor_tensor, T.ex[:, 8:16], T.ts[:, 0:MX:32], T.ts[:, 16:MX:32], ALU.add)
+            for k in range(4):
+                evx = D("y", [ex], "evx", T.er[0:32, 16 * k:16 * k + 16], T.ex[32 * k:32 * k + 32, :])
+
+    def y_out(i, on_v):
+        o, p = T.ysb[:, PW * i:PW * i + PW], T.py[:, 512 * i:512 * i + PW]
+        t = V([mm[i]], v.tensor_copy, o, p) if on_v else S([mm[i]], o, p, ACT.Copy)
+        D("y", [t], "sto", T.y[:, PW * i:PW * i + PW], o)
+
+    y_out(0, True)
+    y_out(1, False)
+    y_out(2, False)
+    y_out(3, True)
+    for k in range(4):
+        D("s", [pl], "sto", T.osc[4 * k:4 * k + 4, :], T.afts[32 * k:32 * k + 4, :])
+
+    z5 = V([], v.memset, T.e1[0:32, :], 0.0)
+    kk1 = V([c_kk], v.tensor_scalar, T.kk1[0:16, :], T.kk0[0:16, :], MX - 1, None, ALU.bitwise_and)
+    f7 = V([c_p], v.tensor_scalar, T.pf[:, 6:7], T.pi[:, 0:1], 8, None, ALU.is_lt)
+    kk = V([kk1], v.tensor_copy, T.kk[0:16, :], T.kk1[0:16, :])
+    em = V([kk, incl], v.tensor_scalar, T.em[0:16, :], T.kk[0:16, :], T.incl[0:16, NR * CAP - 1:NR * CAP], None, ALU.is_lt)
+    eg = V([em, f7], v.tensor_scalar, T.eg[0:16, :], T.em[0:16, :], -1.0, T.pf[0:16, 6:7], ALU.add, ALU.mult)
     e0 = V([evx], v.tensor_tensor, T.e0[0:32, :], T.er[0:32, 0:32], T.er[0:32, 32:64], ALU.add)
     e1 = V([e0, z5], v.tensor_tensor, T.e1[0:32, 0:16], T.e0[0:32, 0:16], T.e0[0:32, 16:32], ALU.add)
     e2 = V([e1], v.transpose, T.e2[0:32, :], T.e1[0:32, :])
     e3 = V([e2, em], v.tensor_tensor, T.e3[0:16, :], T.e2[0:16, :], T.em[0:16, :], ALU.mult)
     e4 = V([e3, eg], v.tensor_tensor, T.e4[0:16, :], T.e3[0:16, :], T.eg[0:16, :], ALU.add)
-    for i in range(NP):
-        o, p = T.ysb[:, PW * i:PW * i + PW], T.py[:, 512 * i:512 * i + PW]
-        yc = S([mm[i]], o, p, ACT.Copy) if i < NP - 1 else V([mm[i]], v.tensor_copy, o, p)
-        D("y", [yc], "sto", T.y[:, PW * i:PW * i + PW], o)
-    for k in range(4):
-        D("s", [pl], "sto", T.osc[4 * k:4 * k + 4, :], T.afts[32 * k:32 * k + 4, :])
     D("s", [e4], "sto", T.ev[:], T.e4[0:16, :])
 
     for name in SEMAPHORES:

@@ -5,6 +5,7 @@ NR, NT, NC, CAP, MX = 4, 512, 1024, 96, 256
 NW = NC + NR * CAP
 LC = CAP // 16
 BLK = [0, 4, 1, 5, 2, 6, 3, 7]
+HN = 256
 TINY = 2.0 ** -120
 NP, PW = 4, 256
 
@@ -14,10 +15,10 @@ _SPEC = {
     "uint8": "us 272 xs 512 wsc 128 snds 384 wins 1408 afts 1024",
     "int32": "sn8 24 ll 24 pi 8 pa 16 vo0 8 kk0 32 kk1 32",
     "uint16": "su 24 lu 24 rkd 16 rkn 8 off 64 vo 8 pm 4 ud 8",
-    "bfloat16": "u0 16 ua 1088 xt 2048 wt 512 eq 1024 eqm 1024 w01 528 csg 768 cm3 512 cm4 1024 cm5 1024 cm6 1024 cm7 1024 sg0 1024 sg1 1024 sg2 1024 sg3 512",
+    "bfloat16": "u0 16 ua 1088 xt 2048 wt 512 eq 1024 eqm 1024 w01 528 csg 768 cm3 1024 cm4 1024 cm5 1024 cm6 1024 cm7 1024 sg0 1024 sg1 1024 sg2 1024 sg3 512",
     "float16": "co 512 scn 2560",
-    "float32": "df0 1024 df1 1024 df2 1024 df3 512 scol 8 nscol 8 acc1 8 acc2 8 ub 8 ub2 8 ub3 8 cnt 8 fl 384 incl 384 csum 2 ksl 2 kfl 2 a2 64 b2 64 "
-               "pos 1024 pt 256 it 64 tt 64 ysb 1024 pf 8 kcol 2 kcoh 2 js0 256 js 256 vj0 128 vj 128 vs 128 pm0 4 kk 32 "
+    "float32": "df0 1024 df1 1024 df2 1024 df3 512 scol 8 nscol 8 acc1 8 acc2 8 base 8 cnt 8 fl 384 incl 384 csum 2 ksl 2 kfl 2 a2 64 b2 64 "
+               "pos 264 pt 256 it 64 tt 64 ysb 1024 pf 8 kcol 2 kcoh 2 js0 256 js 256 vj0 128 vj 128 vs 128 pm0 4 kk 32 "
                "sr 1024 ej 1024 es 1024 tj 256 ts 256 ex 16 er 64 e0 32 e1 32 e2 32 e3 32 e4 32 em 32 eg 32",
 }
 for _d in _SPEC:
@@ -74,11 +75,11 @@ def rank_program(g, core, T, topo):
     c_pm = G([], g.iota, T.pm0[:], [[32, 2], [2, 2]], 0, 0, **FL)
     for a in range(4):
         c_k = G([], g.iota, T.kcol[32 * a:32 * a + 32, :], [[32, 2]], 64 * a, 1, **FL)
-    c_kk = G([], g.iota, T.kk0[0:16, :], [[1, 32]], 0, 32)
     c_vo = G([], g.iota, T.vo0[:], [[128, 4], [512, 2]], 0, 1)
+    c_vj = G([], g.iota, T.vj0[:], [[128, 4], [512, 2], [1, 16]], 0, 0, **FL)
     for b in range(4):
         c_js = G([], g.iota, T.js0[:, 64 * b:64 * b + 64], [[512, 2], [0, 2], [1, 16]], 128 * b, 0, **FL)
-    c_vj = G([], g.iota, T.vj0[:], [[128, 4], [512, 2], [1, 16]], 0, 0, **FL)
+    c_kk = G([], g.iota, T.kk0[0:16, :], [[1, 32]], 0, 32)
 
     others = [d for d in range(NR) if d != me]
     emask = {d: sum(1 << e for e in topo.engines(core, T.cores[d])[2 * i:2 * i + 2]) for i, d in enumerate(others)}
@@ -105,7 +106,6 @@ def rank_program(g, core, T, topo):
     V([], v.tensor_scalar, T.pa[:, 0:1], T.pi[:, 0:1], 15, None, ALU.bitwise_and)
     a4 = V([], v.tensor_scalar, T.pa[:, 3:4], T.pi[:, 0:1], 3, 1, ALU.logical_shift_right, ALU.bitwise_and)
     z4 = V([], v.memset, T.acc1[:], 0.0)
-    z4 = V([], v.memset, T.acc2[:], 0.0)
     f4 = V([a4], v.tensor_copy, T.pf[:, 0:4], T.pa[:, 0:4])
     z1 = V([], v.memset, T.w01[:], 1.0)
     V([u0, z_u], v.tensor_copy, T.ua[:, 4 * 142:4 * 143], T.u0[:, 0:4])
@@ -116,8 +116,10 @@ def rank_program(g, core, T, topo):
     z2 = V([z1], v.memset, T.w01[:, 0:1], 0.0)
     f5 = V([f4], v.tensor_scalar, T.pf[:, 4:5], T.pf[:, 2:3], 4.0, None, ALU.mult)
     kc = V([c_k], v.tensor_scalar, T.kcoh[:], T.kcol[:], 0.5, None, ALU.add)
+    vo = V([c_vo], v.tensor_copy, T.vo[:], T.vo0[:])
     f6 = V([f5], v.tensor_tensor, T.pf[:, 5:6], T.pf[:, 4:5], T.pf[:, 3:4], ALU.add)
     z3 = V([], v.memset, T.a2[:], 0.0)
+    z8 = V([], v.memset, T.pos[:, MX:MX + 8], 0.0)
     pm = V([f6, c_pm], v.tensor_scalar, T.pm[:], T.pm0[:], T.pf[:, 5:6], None, ALU.add)
 
     def rows(ps, h):
@@ -147,18 +149,18 @@ def rank_program(g, core, T, topo):
         return S([rs[a // 512], rs[(b - 1) // 512], nsc[i % 2]], T["df%d" % i][:, a:b], T.pss[:, a:b], ACT.Identity, bias=T.nscol[:, i:i + 1])
 
     def s_sign(i, d, n=NC):
-        b, df, sg, t = min(128 * BLK[i], n), T["df%d" % i], T["sg%d" % i], None
+        b, df, sg, t = min(128 * BLK[i], n), T["df%d" % i], T["sg%d" % i], []
         if b:
-            t = S([d, z4], sg[:, 0:b], df[:, 0:b], ACT.Sign, bias=TINY, scale=-1.0, accum_out=T.acc1[:, i:i + 1])
+            t.append(S([d, z4], sg[:, 0:b], df[:, 0:b], ACT.Sign, bias=TINY, scale=-1.0, accum_out=T.acc1[:, i:i + 1]))
         if b < n:
-            t = S([d, z4], sg[:, b:n], df[:, b:n], ACT.Sign, bias=-TINY, scale=-1.0, accum_out=T.acc2[:, i:i + 1])
+            t.append(S([d], sg[:, b:n], df[:, b:n], ACT.Sign, bias=-TINY, scale=-1.0, accum_out=T.acc2[:, i:i + 1]))
         return t
 
     def v_cmp(i, a, b, o=0):
         m, cm, t = min(max(128 * BLK[i], a), b), T["cm%d" % i], None
         for lo, hi, op in ((a, m, ALU.is_le), (m, b, ALU.is_lt)):
             if lo < hi:
-                t = V([rv[lo // 512], rv[(hi - 1) // 512], sc[i % 2]], v.tensor_scalar, cm[:, lo - o:hi - o], T.psv[:, lo:hi], T.scol[:, i:i + 1], None, op)
+                t = V([rv[lo // 512], rv[(hi - 1) // 512], sc[i % 2]], v.tensor_scalar, cm[:, lo - o:hi - o], T.psv[:, lo:hi], T.scol[:, i:i + 1], 2.0, op, ALU.mult)
         return t
 
     def v_sum(i, c, n=NC, init=0.0):
@@ -168,10 +170,11 @@ def rank_program(g, core, T, topo):
     def v_eq(h):
         for i in range(h, 8, 2):
             b = 128 * BLK[i]
-            t = V([sc[h], rv[h]], v.tensor_scalar, T.eq[:, 128 * i:128 * i + 128], T.psv[:, b:b + 128], T.scol[:, i:i + 1], None, ALU.is_equal)
+            t = V([sc[h], rv[h]], v.tensor_scalar, T.eq[:, 128 * i:128 * i + 128], T.psv[:, b:b + 128], T.scol[:, i:i + 1], 2.0, ALU.is_equal, ALU.mult)
         return t
 
     columns(0)
+    js = V([c_js, f4], v.tensor_scalar, T.js[:], T.js0[:], T.pf[:, 1:2], None, ALU.add)
     s_diff(0, 0, 512)
     v_eq(0)
     s_diff(2, 0, 512)
@@ -192,59 +195,61 @@ def rank_program(g, core, T, topo):
     carr = tick("carr", 4 * len(others))
     D("y", [pq], "own", T.winq[:, w0:w0 + CAP].bitcast(u8), T.sndq[:, own0:own0 + CAP].bitcast(u8))
     own = D("y", [ps], "own", T.wins[:, w0:w0 + CAP], T.snds[:, own0:own0 + CAP])
+    z6 = G([], g.iota, T.ej[:, 0:MX], [[0, MX]], 0, 0, **FL)
+    z7 = G([], g.iota, T.es[:, 0:MX], [[0, MX]], 0, 0, **FL)
 
     v_sum(4, c4)
     d2 = s_diff(2, 512, 1024)
-    z8 = V([], v.memset, T.pos[:, MX:NC], 0.0)
     lu = V([larr, lown], v.tensor_scalar, T.lu[:], T.ll[:], 1.0, None, ALU.add)
     fl = S([lu, z2], T.fl[:], T.w01[:].indirect(T.lu[:]), ACT.Copy)
     s_sign(2, d2)
-    c3 = v_cmp(3, 512, 1024, 512)
+    c3 = v_cmp(3, HN, 1024, HN)
     v_sum(6, c6)
     incl = V([fl], v.tensor_tensor_scan, T.incl[:], T.fl[:], T.fl[:], 0.0, ALU.add, ALU.max)
-    d1 = s_diff(1, 0, 1024)
-    c5 = v_cmp(5, 0, 1024)
     for h in range(2):
         cs = S([incl, kc], T.csg[:, 384 * h:384 * h + 384], T.incl[:], ACT.Sign, bias=T.kcoh[:, h:h + 1], scale=-1.0, accum_out=T.csum[:, h:h + 1])
-    s_sign(1, d1)
-    sg = s_sign(3, s_diff(3, 0, 512), 512)
-    v_sum(3, c3, 512, -256.0)
+    d3 = s_diff(3, 0, HN)
+    d1 = s_diff(1, 0, 1024)
+    c5 = v_cmp(5, 0, 1024)
+    s_sign(3, d3, HN)
+    s1, s2 = s_sign(1, d1)
+    v_sum(3, c3, NC - HN, float(HN))
     for i in range(8):
         a = 128 * i
-        co = V([eqm], v.tensor_tensor_scan, T.co[:, 64 * i:64 * i + 64], T.eqm[:, a:a + 64], T.eqm[:, a + 64:a + 128], 0.0, ALU.add, ALU.add)
-    js = V([c_js, f4], v.tensor_scalar, T.js[:], T.js0[:], T.pf[:, 1:2], None, ALU.add)
+        co = V([eqm], v.tensor_tensor_scan, T.co[:, 64 * i:64 * i + 64], T.eqm[:, a:a + 64], T.eqm[:, a + 64:a + 128], float(NC) if i < 3 else 0.0, ALU.add, ALU.add)
     sl = V([cs], v.tensor_scalar, T.ksl[:], T.csum[:], 0.5, float(NC + NR * CAP // 2), ALU.mult, ALU.add)
     v_sum(5, c5)
     kf = V([sl], v.tensor_scalar, T.kfl[:], T.ksl[:], float(NW), None, ALU.is_lt)
-    ub = V([co], v.tensor_scalar, T.ub[:, 0:4], T.co[:, 63:64 * 4:64], 2.0, 1024.0, ALU.mult, ALU.add)
+    vj = V([c_vj], v.tensor_scalar, T.vj[:], T.vj0[:], T.pf[:, 1:2], None, ALU.add)
     km = V([kf, z3], v.tensor_tensor, T.a2[:, 0:64:32], T.ksl[:], T.kfl[:], ALU.mult)
-    V([co], v.tensor_copy, T.cnt[:, 4:8], T.co[:, 64 * 4 + 63:512:64])
+    c7 = v_cmp(7, 0, 128 * BLK[7])
     b2 = V([km], v.transpose, T.b2[:], T.a2[:])
     for a in range(4):
         pos = G([b2], g.partition_broadcast, T.pos[:, 64 * a:64 * a + 64], T.b2[32 * a:32 * a + 1, :], 128)
-    c7 = v_cmp(7, 0, 1024)
-    ub2 = V([ub, sg], v.tensor_tensor, T.ub2[:, 0:4], T.ub[:, 0:4], T.acc1[:, 0:4], ALU.add)
+    c7 = v_cmp(7, 128 * BLK[7], 1024)
+    bs = V([s1, co], v.tensor_tensor, T.base[:], T.co[:, 63:512:64], T.acc1[:], ALU.add)
     sm = v_sum(7, c7)
-    ub3 = V([ub2], v.tensor_tensor, T.ub3[:, 0:4], T.ub2[:, 0:4], T.acc2[:, 0:4], ALU.add)
-    cn = V([ub3], v.tensor_scalar, T.cnt[:, 0:4], T.ub3[:, 0:4], 0.5, None, ALU.mult)
+    V([s2, bs], v.tensor_tensor, T.cnt[:, 0:3], T.base[:, 0:3], T.acc2[:, 0:3], ALU.add)
+    cn = V([sm], v.tensor_tensor, T.cnt[:, 3:8], T.scn[:, 511:2560:512], T.base[:, 3:8], ALU.add)
 
-    cn = V([sm, cn], v.tensor_tensor, T.cnt[:, 3:8], T.scn[:, 511:2560:512], T.cnt[:, 3:8], ALU.add)
-    V([cn], v.tensor_copy, T.rkd[:, 0:16:2], T.cnt[:])
-    rd = V([], v.tensor_copy, T.rkd[:, 1:16:2], T.cnt[:])
+    V([cn], v.tensor_scalar, T.rkd[:, 0:16:2], T.cnt[:], 0.5, float(MX), ALU.mult, ALU.min)
+    rd = V([], v.tensor_scalar, T.rkd[:, 1:16:2], T.cnt[:], 0.5, float(MX), ALU.mult, ALU.min)
     pt = V([rd, pos, z8, js], v.tensor_tensor, T.pt[:], T.pos[:].indirect(T.rkd[:]), T.js[:], ALU.max)
     for a in range(4):
         hop = D("y", [pt], "hop", T.it[32 * a:32 * a + 32, :], T.pt[a:128:16, :])
 
     sr = S([], T.sr[:], T.pss[:], ACT.Copy)
-    vo = V([c_vo], v.tensor_copy, T.vo[:], T.vo0[:])
     vs = S([sr, vo], T.vs[:], T.sr[:].indirect(T.vo[:]), ACT.Copy)
-    rn = V([], v.tensor_copy, T.rkn[:], T.cnt[:])
-    vj = V([c_vj], v.tensor_scalar, T.vj[:], T.vj0[:], T.pf[:, 1:2], None, ALU.add)
-    z6 = V([], v.memset, T.ej[:, 0:MX], 0.0)
-    z7 = V([], v.memset, T.es[:, 0:MX], 0.0)
-    ej = V([rn, z6, vj], v.tensor_copy, T.ej[:].indirect(T.rkn[:]), T.vj[:])
+    rn = V([], v.tensor_scalar, T.rkn[:], T.cnt[:], 0.5, None, ALU.mult)
     wq = V([wl], v.quantize_mx, T.wq[:], T.wsc[:], T.wt[:])
+    ej = V([rn, z6, vj], v.tensor_copy, T.ej[:].indirect(T.rkn[:]), T.vj[:])
     es = V([vs, z7], v.tensor_copy, T.es[:].indirect(T.rkn[:]), T.vs[:])
+    tj = V([ej], v.transpose, T.tj[:], T.ej[:, 0:MX])
+    ts = V([es], v.transpose, T.ts[:], T.es[:, 0:MX])
+    V([tj], v.tensor_tensor, T.ex[:, 0:8], T.tj[:, 0:MX:32], T.tj[:, 16:MX:32], ALU.add)
+    ex = V([ts], v.tensor_tensor, T.ex[:, 8:16], T.ts[:, 0:MX:32], T.ts[:, 16:MX:32], ALU.add)
+    for a in range(4):
+        evx = D("y", [ex], "evx", T.er[0:32, 16 * a:16 * a + 16], T.ex[32 * a:32 * a + 32, :])
 
     tt = V([hop], v.transpose, T.tt[:], T.it[:])
     off = V([tt, pm], v.tensor_copy, T.off[:], T.tt[:].indirect(T.pm[:]))
@@ -256,14 +261,6 @@ def rank_program(g, core, T, topo):
         pl = S([off, k0, k1, own, carr], T.afts[:, a:b], T.wins[:].indirect(o), ACT.Copy)
         mm.append(P([t, pl, wq, sc[1]], T.py[:, 512 * i:512 * i + PW], T.wq[:], T.wsc[:], T.aftq[:, a:b], T.afts[:, a:b], True, True))
         D("y", [t], "sto", T.oc[:, 4 * a:4 * b], T.aftq[:, a:b].bitcast(u8))
-        if i == 0:
-            tj = V([ej], v.transpose, T.tj[:], T.ej[:, 0:MX])
-            ts = V([es], v.transpose, T.ts[:], T.es[:, 0:MX])
-        if i == 1:
-            V([tj], v.tensor_tensor, T.ex[:, 0:8], T.tj[:, 0:MX:32], T.tj[:, 16:MX:32], ALU.add)
-            ex = V([ts], v.tensor_tensor, T.ex[:, 8:16], T.ts[:, 0:MX:32], T.ts[:, 16:MX:32], ALU.add)
-            for k in range(4):
-                evx = D("y", [ex], "evx", T.er[0:32, 16 * k:16 * k + 16], T.ex[32 * k:32 * k + 32, :])
 
     def y_out(i, on_v):
         o, p = T.ysb[:, PW * i:PW * i + PW], T.py[:, 512 * i:512 * i + PW]
@@ -271,22 +268,22 @@ def rank_program(g, core, T, topo):
         D("y", [t], "sto", T.y[:, PW * i:PW * i + PW], o)
 
     y_out(0, True)
-    y_out(1, False)
+    kk1 = V([c_kk], v.tensor_scalar, T.kk1[0:16, :], T.kk0[0:16, :], MX - 1, None, ALU.bitwise_and)
+    y_out(1, True)
     y_out(2, False)
+    e0 = V([evx], v.tensor_tensor, T.e0[0:32, :], T.er[0:32, 0:32], T.er[0:32, 32:64], ALU.add)
+    z5 = V([], v.memset, T.e1[0:32, :], 0.0)
     y_out(3, True)
     for k in range(4):
         D("s", [pl], "sto", T.osc[4 * k:4 * k + 4, :], T.afts[32 * k:32 * k + 4, :])
 
-    z5 = V([], v.memset, T.e1[0:32, :], 0.0)
-    kk1 = V([c_kk], v.tensor_scalar, T.kk1[0:16, :], T.kk0[0:16, :], MX - 1, None, ALU.bitwise_and)
-    f7 = V([c_p], v.tensor_scalar, T.pf[:, 6:7], T.pi[:, 0:1], 8, None, ALU.is_lt)
-    kk = V([kk1], v.tensor_copy, T.kk[0:16, :], T.kk1[0:16, :])
-    em = V([kk, incl], v.tensor_scalar, T.em[0:16, :], T.kk[0:16, :], T.incl[0:16, NR * CAP - 1:NR * CAP], None, ALU.is_lt)
-    eg = V([em, f7], v.tensor_scalar, T.eg[0:16, :], T.em[0:16, :], -1.0, T.pf[0:16, 6:7], ALU.add, ALU.mult)
-    e0 = V([evx], v.tensor_tensor, T.e0[0:32, :], T.er[0:32, 0:32], T.er[0:32, 32:64], ALU.add)
     e1 = V([e0, z5], v.tensor_tensor, T.e1[0:32, 0:16], T.e0[0:32, 0:16], T.e0[0:32, 16:32], ALU.add)
+    kk = V([kk1], v.tensor_copy, T.kk[0:16, :], T.kk1[0:16, :])
+    f7 = V([c_p], v.tensor_scalar, T.pf[:, 6:7], T.pi[:, 0:1], 8, None, ALU.is_lt)
     e2 = V([e1], v.transpose, T.e2[0:32, :], T.e1[0:32, :])
+    em = V([kk, incl], v.tensor_scalar, T.em[0:16, :], T.kk[0:16, :], T.incl[0:16, NR * CAP - 1:NR * CAP], None, ALU.is_lt)
     e3 = V([e2, em], v.tensor_tensor, T.e3[0:16, :], T.e2[0:16, :], T.em[0:16, :], ALU.mult)
+    eg = V([em, f7], v.tensor_scalar, T.eg[0:16, :], T.em[0:16, :], -1.0, T.pf[0:16, 6:7], ALU.add, ALU.mult)
     e4 = V([e3, eg], v.tensor_tensor, T.e4[0:16, :], T.e3[0:16, :], T.eg[0:16, :], ALU.add)
     D("s", [e4], "sto", T.ev[:], T.e4[0:16, :])
 

@@ -4,28 +4,31 @@ from concourse.mybir import dt, AluOpType as ALU, ActivationFunctionType as ACT
 NR, NT, NC, CAP, MX = 4, 512, 1024, 96, 256
 NW = NC + NR * CAP
 LC = CAP // 16
-BLK = [0, 4, 1, 5, 2, 6, 3, 7]
-HN = 256
+BLK = [3, 7, 2, 6, 1, 5, 0, 4]
+NS = 3
+VP, SP = [[4, 6], [3, 5, 7]], [[0, 2], [1]]
+WD = NC + 128
 TINY = 2.0 ** -120
 NP, PW = 4, 256
+UC = 14
 
 SCRATCH = {"psv": ("psum", [128, 1024], "float32"), "pss": ("psum", [128, 1024], "float32"), "py": ("psum", [128, 2048], "float32")}
 _SPEC = {
-    "float8_e4m3fn_x4": "uq 272 xq 512 wq 128 sndq 384 winq 1408 aftq 1024",
-    "uint8": "us 272 xs 512 wsc 128 snds 384 wins 1408 afts 1024",
-    "int32": "sn8 24 ll 24 pi 8 pa 16 vo0 8 kk0 32 kk1 32",
-    "uint16": "su 24 lu 24 rkd 16 rkn 8 off 64 vo 8 pm 4 ud 8",
-    "bfloat16": "u0 16 ua 1088 xt 2048 wt 512 eq 1024 eqm 1024 w01 528 csg 768 cm3 1024 cm4 1024 cm5 1024 cm6 1024 cm7 1024 sg0 1024 sg1 1024 sg2 1024 sg3 512",
-    "float16": "co 512 scn 2560",
-    "float32": "df0 1024 df1 1024 df2 1024 df3 512 scol 8 nscol 8 acc1 8 acc2 8 base 8 cnt 8 fl 384 incl 384 csum 2 ksl 2 kfl 2 a2 64 b2 64 "
-               "pos 264 pt 256 it 64 tt 64 ysb 1024 pf 8 kcol 2 kcoh 2 js0 256 js 256 vj0 128 vj 128 vs 128 pm0 4 kk 32 "
-               "sr 1024 ej 1024 es 1024 tj 256 ts 256 ex 16 er 64 e0 32 e1 32 e2 32 e3 32 e4 32 em 32 eg 32",
+    "float8_e4m3fn_x4": "uq 144 urq 128 xq 512 wq 128 sndq 384 winq 1408 aftq 1024",
+    "uint8": "us 144 urs 128 xs 512 wsc 128 snds 384 wins 1408 afts 1024",
+    "int32": "sn8 24 ll 24 pi 8 pa 2 vo0 8 kk0 16 kk1 16",
+    "uint16": "su 24 lu 24 ul 8 rkd 16 rkn 8 off 64 vo 8 pm 4",
+    "bfloat16": "u0 16 ua 576 xt 2048 wt 512 eq 1024 eqm 384 w01 528 fl 384 incl 384 csg 768 cm3 1152 cm4 1152 cm5 1152 cm6 1152 cm7 1152 sg0 1024 sg1 1024 sg2 1024",
+    "float16": "co 192 scn 4608",
+    "float32": "df0 1024 df1 1024 df2 1024 scol 8 acc1 4 acc2 4 base 4 csum 2 ksl 2 kfl 2 a2 64 b2 64 "
+               "pos 264 pt 256 it 64 tt 64 ysb 1024 pf 2 kcol 2 kcoh 2 js 256 vj 128 vs 128 pm0 4 kk 16 "
+               "sr 1024 ej 1024 es 1024 er 128 e0 64 e1 32 e2 16 e3 16 e4 16 em 16 eg 16",
 }
 for _d in _SPEC:
     _w = _SPEC[_d].split()
     for _i in range(0, len(_w), 2):
         SCRATCH[_w[_i]] = ("sbuf", [128, int(_w[_i + 1])], _d)
-SEMAPHORES = "qv qs qt qg lsn lu0 lk0 lk1 lx lw lown own hop evx sto larr carr sent".split()
+SEMAPHORES = "qv qs qt qg lsn lu0 lk0 lk1 lk2 lx lw lown own hop evx sto larr carr sent".split()
 
 
 def rank_program(g, core, T, topo):
@@ -61,25 +64,26 @@ def rank_program(g, core, T, topo):
     def D(q, deps, sem, out, in_):
         wait(q, deps); queues[q].dma_start(out, in_).then_inc(T.sem[sem], 16); return tick(sem, 16)
 
-    D("y", [], "lk0", T.winq[:, 0:512].bitcast(u8), T.kc[:, 0:2048])
-    k0 = D("y", [], "lk0", T.wins[:, 0:512], T.ks[:, 0:512])
-    D("y", [], "lk1", T.winq[:, 512:1024].bitcast(u8), T.kc[:, 2048:4096])
-    k1 = D("y", [], "lk1", T.wins[:, 512:1024], T.ks[:, 512:1024])
+    kl = []
+    for i, (a, b) in enumerate(((0, 256), (256, 512), (512, 1024))):
+        D("y", [], "lk%d" % i, T.winq[:, a:b].bitcast(u8), T.kc[:, 4 * a:4 * b])
+        kl.append(D("y", [], "lk%d" % i, T.wins[:, a:b], T.ks[:, a:b]))
     u0 = D("s", [], "lu0", T.u0[:], T.u[:, 0:16])
     for q in range(8):
         sn = D("s" if q < 6 else "y", [], "lsn", T.sn8[16 * q:16 * q + 16, :], T.sn[:])
     xl = D("y", [], "lx", T.xt[:], T.x[:])
     wl = D("y", [], "lw", T.wt[:], T.w[:])
 
-    c_p = G([], g.iota, T.pi[:], [[0, 8]], 0, 1)
-    c_pm = G([], g.iota, T.pm0[:], [[32, 2], [2, 2]], 0, 0, **FL)
+    G([], g.iota, T.pi[:, 0:4], [[0, 4]], 0, 1)
+    c_p = G([], g.iota, T.pi[:, 4:8], [[0, 4]], 0, 4)
+    c_pm = G([], g.iota, T.pm0[:], [[32, 2], [-2, 2]], 3, 0, **FL)
+    c_kk = G([], g.iota, T.kk0[0:32, :], [[1, 16]], 0, 16)
     for a in range(4):
         c_k = G([], g.iota, T.kcol[32 * a:32 * a + 32, :], [[32, 2]], 64 * a, 1, **FL)
-    c_vo = G([], g.iota, T.vo0[:], [[128, 4], [512, 2]], 0, 1)
-    c_vj = G([], g.iota, T.vj0[:], [[128, 4], [512, 2], [1, 16]], 0, 0, **FL)
+    c_vo = G([], g.iota, T.vo0[:], [[-128, 4], [512, 2]], 384, 1)
     for b in range(4):
-        c_js = G([], g.iota, T.js0[:, 64 * b:64 * b + 64], [[512, 2], [0, 2], [1, 16]], 128 * b, 0, **FL)
-    c_kk = G([], g.iota, T.kk0[0:16, :], [[1, 32]], 0, 32)
+        c_js = G([], g.iota, T.js[:, 64 * b:64 * b + 64], [[512, 2], [0, 2], [1, 16]], 384 - 128 * b, 1, **FL)
+    c_vj = G([], g.iota, T.vj[:], [[-128, 4], [512, 2], [1, 16]], 384, 1, **FL)
 
     others = [d for d in range(NR) if d != me]
     emask = {d: sum(1 << e for e in topo.engines(core, T.cores[d])[2 * i:2 * i + 2]) for i, d in enumerate(others)}
@@ -98,93 +102,104 @@ def rank_program(g, core, T, topo):
     larr = tick("larr", 2 * len(others))
     lown = D("y", [sn], "lown", T.ll[:, LC * me:LC * me + LC], T.sn8[:, LC * me:LC * me + LC])
 
-    z_u = V([], v.memset, T.ua[:, 512:1088], 0.0)
-    a8 = V([c_p], v.tensor_scalar, T.pa[:, 8:16], T.pi[:], 3, None, ALU.bitwise_and)
-    V([], v.tensor_scalar, T.pa[:, 1:2], T.pi[:, 0:1], 112, None, ALU.bitwise_and)
-    ud = V([a8], v.tensor_copy, T.ud[:], T.pa[:, 8:16])
-    V([], v.tensor_scalar, T.pa[:, 2:3], T.pi[:, 0:1], 7, None, ALU.bitwise_and)
-    V([], v.tensor_scalar, T.pa[:, 0:1], T.pi[:, 0:1], 15, None, ALU.bitwise_and)
-    a4 = V([], v.tensor_scalar, T.pa[:, 3:4], T.pi[:, 0:1], 3, 1, ALU.logical_shift_right, ALU.bitwise_and)
-    z4 = V([], v.memset, T.acc1[:], 0.0)
-    f4 = V([a4], v.tensor_copy, T.pf[:, 0:4], T.pa[:, 0:4])
-    z1 = V([], v.memset, T.w01[:], 1.0)
-    V([u0, z_u], v.tensor_copy, T.ua[:, 4 * 142:4 * 143], T.u0[:, 0:4])
-    t = V([ud], v.tensor_copy, T.ua[:, 0:128], T.u0[:].indirect(T.ud[:]))
-    t = V([t], v.tensor_copy, T.ua[:, 128:256], T.ua[:, 0:128])
-    t = V([t], v.tensor_copy, T.ua[:, 256:512], T.ua[:, 0:256])
+    z_u = V([], v.memset, T.ua[:], 0.0)
+    z_l = V([], v.memset, T.ul[:], UC)
+    t = V([u0, z_u], v.tensor_copy, T.ua[:, 4 * UC:4 * UC + 4], T.u0[:, 0:4])
     uq = V([t], v.quantize_mx, T.uq[:], T.us[:], T.ua[:])
-    z2 = V([z1], v.memset, T.w01[:, 0:1], 0.0)
-    f5 = V([f4], v.tensor_scalar, T.pf[:, 4:5], T.pf[:, 2:3], 4.0, None, ALU.mult)
+    ur = V([uq, z_l], v.tensor_copy, T.urq[:].bitcast(u32), T.uq[:].bitcast(u32).indirect(T.ul[:]))
+    S([z_u], T.w01[:, 1:513], T.ua[:, 64:576], ACT.Identity, bias=1.0, scale=0.0)
+    us = S([uq, z_l], T.urs[:], T.us[:].indirect(T.ul[:]), ACT.Copy)
+    z2 = S([], T.w01[:, 0:1], T.ua[:, 64:65], ACT.Copy)
+    z3 = S([], T.a2[:], T.ua[:, 64:128], ACT.Copy)
+    z8 = S([], T.pos[:, MX:MX + 8], T.ua[:, 64:72], ACT.Copy)
+    V([c_p], v.tensor_scalar, T.pa[:, 0:1], T.pi[:, 4:5], 28, None, ALU.bitwise_and)
+    a2 = V([], v.tensor_scalar, T.pa[:, 1:2], T.pi[:, 0:1], 3, 1, ALU.logical_shift_right, ALU.bitwise_and)
+    f7 = V([], v.tensor_scalar, T.pf[:, 1:2], T.pi[:, 0:1], 16, None, ALU.is_lt)
+    f6 = V([a2], v.tensor_tensor, T.pf[:, 0:1], T.pa[:, 0:1], T.pa[:, 1:2], ALU.subtract)
+    kk1 = V([c_kk], v.tensor_scalar, T.kk1[0:32, :], T.kk0[0:32, :], MX - 1, None, ALU.bitwise_and)
+    pm = V([f6, c_pm], v.tensor_scalar, T.pm[:], T.pm0[:], T.pf[:, 0:1], None, ALU.add)
+    kk = V([kk1], v.tensor_copy, T.kk[0:32, :], T.kk1[0:32, :])
     kc = V([c_k], v.tensor_scalar, T.kcoh[:], T.kcol[:], 0.5, None, ALU.add)
-    vo = V([c_vo], v.tensor_copy, T.vo[:], T.vo0[:])
-    f6 = V([f5], v.tensor_tensor, T.pf[:, 5:6], T.pf[:, 4:5], T.pf[:, 3:4], ALU.add)
-    z3 = V([], v.memset, T.a2[:], 0.0)
-    z8 = V([], v.memset, T.pos[:, MX:MX + 8], 0.0)
-    pm = V([f6, c_pm], v.tensor_scalar, T.pm[:], T.pm0[:], T.pf[:, 5:6], None, ALU.add)
 
     def rows(ps, h):
         a, b = 512 * h, 512 * h + 512
-        return P([], ps[:, a:b], T.uq[:, 0:128], T.us[:, 0:128], T.winq[:, a:b], T.wins[:, a:b], True, True)
+        return P([ur, us, kl[h + 1]], ps[:, a:b], T.urq[:], T.urs[:], T.winq[:, a:b], T.wins[:, a:b], True, True)
 
-    def cols(h, deps):
-        for i in range(h, 8, 2):
-            b, o = 128 * BLK[i], 142 - 2 * i
-            t = P(deps, T.py[:, 512 * h:512 * h + 128], T.winq[:, b:b + 128], T.wins[:, b:b + 128], T.uq[:, o:o + 128], T.us[:, o:o + 128], i == h, i == h + 6)
-        return t
+    sc = {}
 
-    pc = [cols(0, [uq, k0])]
-    rv = [rows(T.psv, 0)]
-    rs = [rows(T.pss, 0)]
-    pc.append(cols(1, [k1]))
+    def cols(bank, places, dep):
+        for i in places:
+            b, o = 128 * BLK[i], UC - 2 * i
+            sc[i] = P([uq, dep], T.py[:, 512 * bank:512 * bank + 128], T.winq[:, b:b + 128], T.wins[:, b:b + 128],
+                      T.uq[:, o:o + 128], T.us[:, o:o + 128], i == places[0], i == places[-1])
+
+    rv, rs = [], []
+    cols(0, VP[0], kl[0])
+    rv.append(rows(T.psv, 0))
+    cols(1, SP[0], kl[1])
+    rs.append(rows(T.pss, 0))
+    cols(2, VP[1], kl[2])
     rv.append(rows(T.psv, 1))
+    cols(3, SP[1], kl[2])
     rs.append(rows(T.pss, 1))
-    nsc, sc = [], []
 
-    def columns(h):
-        p = T.py[:, 512 * h + 2 * h:512 * h + 16:4]
-        nsc.append(V([pc[h]], v.tensor_scalar, T.nscol[:, h:8:2], p, -1.0, None, ALU.mult))
-        sc.append(V([pc[h]], v.tensor_copy, T.scol[:, h:8:2], p))
+    def columns(h, on_v):
+        places, bank = (VP if on_v else SP)[h], 512 * (2 * h + (not on_v))
+        i, j = places[0], places[-1] + 1
+        o, p, d = T.scol[:, i:j:2], T.py[:, bank + 2 * i:bank + 2 * j:4], [sc[places[-1]]]
+        t = V(d, v.tensor_copy, o, p) if on_v else S(d, o, p, ACT.Copy)
+        for k in places:
+            sc[k] = t
 
     def s_diff(i, a, b):
-        return S([rs[a // 512], rs[(b - 1) // 512], nsc[i % 2]], T["df%d" % i][:, a:b], T.pss[:, a:b], ACT.Identity, bias=T.nscol[:, i:i + 1])
+        return S([rs[a // 512], rs[(b - 1) // 512], sc[i]], T["df%d" % i][:, a:b], T.pss[:, a:b], ACT.Identity, bias=T.scol[:, i:i + 1], scale=-1.0)
 
-    def s_sign(i, d, n=NC):
-        b, df, sg, t = min(128 * BLK[i], n), T["df%d" % i], T["sg%d" % i], []
-        if b:
-            t.append(S([d, z4], sg[:, 0:b], df[:, 0:b], ACT.Sign, bias=TINY, scale=-1.0, accum_out=T.acc1[:, i:i + 1]))
-        if b < n:
-            t.append(S([d], sg[:, b:n], df[:, b:n], ACT.Sign, bias=-TINY, scale=-1.0, accum_out=T.acc2[:, i:i + 1]))
-        return t
+    def s_sign(i, d):
+        b, df, sg = 128 * BLK[i], T["df%d" % i], T["sg%d" % i]
+        S([d], sg[:, 0:b], df[:, 0:b], ACT.Sign, bias=TINY, accum_out=T.acc1[:, i:i + 1])
+        return S([d], sg[:, b:NC], df[:, b:NC], ACT.Sign, bias=-TINY, accum_out=T.acc2[:, i:i + 1])
 
-    def v_cmp(i, a, b, o=0):
+    def v_cmp(i, a, b):
         m, cm, t = min(max(128 * BLK[i], a), b), T["cm%d" % i], None
         for lo, hi, op in ((a, m, ALU.is_le), (m, b, ALU.is_lt)):
             if lo < hi:
-                t = V([rv[lo // 512], rv[(hi - 1) // 512], sc[i % 2]], v.tensor_scalar, cm[:, lo - o:hi - o], T.psv[:, lo:hi], T.scol[:, i:i + 1], 2.0, op, ALU.mult)
+                t = V([rv[lo // 512], rv[(hi - 1) // 512], sc[i]], v.tensor_scalar, cm[:, lo:hi], T.psv[:, lo:hi], T.scol[:, i:i + 1], 2.0, op, ALU.mult)
         return t
 
-    def v_sum(i, c, n=NC, init=0.0):
-        cm, o = T["cm%d" % i], 512 * (i - 3)
-        return V([c], v.tensor_tensor_scan, T.scn[:, o + 512 - n // 2:o + 512], cm[:, 0:n // 2], cm[:, n // 2:n], init, ALU.add, ALU.add)
+    def v_sum(i, c):
+        cm, o = T["cm%d" % i], WD // 2 * i
+        return V([c, eqm[i]], v.tensor_tensor_scan, T.scn[:, o:o + WD // 2], cm[:, 0:WD // 2], cm[:, WD // 2:WD], 0.0, ALU.add, ALU.add)
 
-    def v_eq(h):
-        for i in range(h, 8, 2):
+    def v_eq(h, places):
+        for i in places:
             b = 128 * BLK[i]
-            t = V([sc[h], rv[h]], v.tensor_scalar, T.eq[:, 128 * i:128 * i + 128], T.psv[:, b:b + 128], T.scol[:, i:i + 1], 2.0, ALU.is_equal, ALU.mult)
-        return t
+            eqt[i] = V([sc[i], rv[h]], v.tensor_scalar, T.eq[:, 128 * i:128 * i + 128], T.psv[:, b:b + 128], T.scol[:, i:i + 1], 2.0, ALU.is_equal, ALU.mult)
 
-    columns(0)
-    js = V([c_js, f4], v.tensor_scalar, T.js[:], T.js0[:], T.pf[:, 1:2], None, ALU.add)
+    def g_eq(i):
+        eqm[i] = G([eqt[i]], g.affine_select, T["cm%d" % i][:, NC:WD], T.eq[:, 128 * i:128 * i + 128], [[-1, 128]], ALU.is_gt, 0.0, 0, 1)
+
+    eqt, eqm = {}, {}
+    columns(0, True)
+    columns(0, False)
     s_diff(0, 0, 512)
-    v_eq(0)
+    v_eq(0, VP[0])
     s_diff(2, 0, 512)
+    for i in VP[0]:
+        g_eq(i)
     v_cmp(4, 0, 512)
     v_cmp(6, 0, 512)
+    v_eq(0, SP[0])
     su = V([sn], v.tensor_copy, T.su[:], T.sn8[:])
-    columns(1)
-    eqm = G([v_eq(1)], g.affine_select, T.eqm[:], T.eq[:], [[0, 8], [-1, 128]], ALU.is_gt, 0.0, 0, 1)
-    s_sign(0, s_diff(0, 512, 1024))
+    columns(1, True)
+    columns(1, False)
+    v_eq(1, VP[1])
+    for i in VP[1]:
+        g_eq(i)
+    d0 = s_diff(0, 512, 1024)
+    s_sign(0, d0)
     c4 = v_cmp(4, 512, 1024)
+    v_eq(1, SP[1])
+    eqs = G([eqt[1]], g.affine_select, T.eqm[:], T.eq[:, 0:128 * NS], [[0, NS], [-1, 128]], ALU.is_gt, 0.0, 0, 1)
     xq = V([xl], v.quantize_mx, T.xq[:], T.xs[:], T.xt[:])
     c6 = v_cmp(6, 512, 1024)
     pq = V([xq, su], v.tensor_copy, T.sndq[:].bitcast(u32), T.xq[:].bitcast(u32).indirect(T.su[:]))
@@ -203,63 +218,64 @@ def rank_program(g, core, T, topo):
     lu = V([larr, lown], v.tensor_scalar, T.lu[:], T.ll[:], 1.0, None, ALU.add)
     fl = S([lu, z2], T.fl[:], T.w01[:].indirect(T.lu[:]), ACT.Copy)
     s_sign(2, d2)
-    c3 = v_cmp(3, HN, 1024, HN)
+    c3 = v_cmp(3, 0, 1024)
     v_sum(6, c6)
     incl = V([fl], v.tensor_tensor_scan, T.incl[:], T.fl[:], T.fl[:], 0.0, ALU.add, ALU.max)
     for h in range(2):
         cs = S([incl, kc], T.csg[:, 384 * h:384 * h + 384], T.incl[:], ACT.Sign, bias=T.kcoh[:, h:h + 1], scale=-1.0, accum_out=T.csum[:, h:h + 1])
-    d3 = s_diff(3, 0, HN)
     d1 = s_diff(1, 0, 1024)
     c5 = v_cmp(5, 0, 1024)
-    s_sign(3, d3, HN)
-    s1, s2 = s_sign(1, d1)
-    v_sum(3, c3, NC - HN, float(HN))
-    for i in range(8):
+    sg = s_sign(1, d1)
+    v_sum(3, c3)
+    co, n64 = {}, float(NC)
+    for i in range(NS):
         a = 128 * i
-        co = V([eqm], v.tensor_tensor_scan, T.co[:, 64 * i:64 * i + 64], T.eqm[:, a:a + 64], T.eqm[:, a + 64:a + 128], float(NC) if i < 3 else 0.0, ALU.add, ALU.add)
-    sl = V([cs], v.tensor_scalar, T.ksl[:], T.csum[:], 0.5, float(NC + NR * CAP // 2), ALU.mult, ALU.add)
-    v_sum(5, c5)
-    kf = V([sl], v.tensor_scalar, T.kfl[:], T.ksl[:], float(NW), None, ALU.is_lt)
-    vj = V([c_vj], v.tensor_scalar, T.vj[:], T.vj0[:], T.pf[:, 1:2], None, ALU.add)
+        co[i] = V([eqs], v.tensor_tensor_scan, T.co[:, 64 * i:64 * i + 64], T.eqm[:, a:a + 64], T.eqm[:, a + 64:a + 128], n64, ALU.add, ALU.add)
+        if i == 0:
+            sl = V([cs], v.tensor_scalar, T.ksl[:], T.csum[:], 0.5, float(NC + NR * CAP // 2), ALU.mult, ALU.add)
+        if i == 1:
+            kf = V([sl], v.tensor_scalar, T.kfl[:], T.ksl[:], float(NW), None, ALU.is_lt)
     km = V([kf, z3], v.tensor_tensor, T.a2[:, 0:64:32], T.ksl[:], T.kfl[:], ALU.mult)
-    c7 = v_cmp(7, 0, 128 * BLK[7])
+    v_sum(5, c5)
     b2 = V([km], v.transpose, T.b2[:], T.a2[:])
     for a in range(4):
         pos = G([b2], g.partition_broadcast, T.pos[:, 64 * a:64 * a + 64], T.b2[32 * a:32 * a + 1, :], 128)
-    c7 = v_cmp(7, 128 * BLK[7], 1024)
-    bs = V([s1, co], v.tensor_tensor, T.base[:], T.co[:, 63:512:64], T.acc1[:], ALU.add)
+    c7 = v_cmp(7, 0, 1024)
     sm = v_sum(7, c7)
-    V([s2, bs], v.tensor_tensor, T.cnt[:, 0:3], T.base[:, 0:3], T.acc2[:, 0:3], ALU.add)
-    cn = V([sm], v.tensor_tensor, T.cnt[:, 3:8], T.scn[:, 511:2560:512], T.base[:, 3:8], ALU.add)
+    last, step = WD // 2 - 1, WD // 2
+    bs = V([sg, co[NS - 1]], v.tensor_tensor, T.base[:, 0:NS], T.co[:, 63:64 * NS:64], T.acc1[:, 0:NS], ALU.add)
+    cn = V([bs], v.tensor_tensor, T.scn[:, last:NS * step:step], T.base[:, 0:NS], T.acc2[:, 0:NS], ALU.add)
+    cnt = T.scn[:, last:8 * step:step]
 
-    V([cn], v.tensor_scalar, T.rkd[:, 0:16:2], T.cnt[:], 0.5, float(MX), ALU.mult, ALU.min)
-    rd = V([], v.tensor_scalar, T.rkd[:, 1:16:2], T.cnt[:], 0.5, float(MX), ALU.mult, ALU.min)
-    pt = V([rd, pos, z8, js], v.tensor_tensor, T.pt[:], T.pos[:].indirect(T.rkd[:]), T.js[:], ALU.max)
+    V([cn, sm], v.tensor_scalar, T.rkd[:, 0:16:2], cnt, 0.5, float(MX), ALU.mult, ALU.min)
+    rd = V([], v.tensor_scalar, T.rkd[:, 1:16:2], cnt, 0.5, float(MX), ALU.mult, ALU.min)
+    rn = V([], v.tensor_scalar, T.rkn[:], cnt, 0.5, None, ALU.mult)
+    pt = V([rd, pos, z8, c_js], v.tensor_tensor, T.pt[:], T.pos[:].indirect(T.rkd[:]), T.js[:], ALU.max)
     for a in range(4):
-        hop = D("y", [pt], "hop", T.it[32 * a:32 * a + 32, :], T.pt[a:128:16, :])
+        hop = D("y", [pt], "hop", T.it[32 * a:32 * a + 32, :], T.pt[0:128:16, :])
 
+    vo = V([c_vo], v.tensor_copy, T.vo[:], T.vo0[:])
     sr = S([], T.sr[:], T.pss[:], ACT.Copy)
     vs = S([sr, vo], T.vs[:], T.sr[:].indirect(T.vo[:]), ACT.Copy)
-    rn = V([], v.tensor_scalar, T.rkn[:], T.cnt[:], 0.5, None, ALU.mult)
+    em = V([kk, incl], v.tensor_scalar, T.em[0:32, :], T.kk[0:32, :], T.incl[0:32, NR * CAP - 1:NR * CAP], None, ALU.is_lt)
+    ej = V([rn, z6, c_vj], v.tensor_copy, T.ej[:].indirect(T.rkn[:]), T.vj[:])
+    for q in range(8):
+        D("s", [ej], "evx", T.er[0:16, 16 * q:16 * q + 16], T.ej[16 * q:16 * q + 1, 0:MX])
     wq = V([wl], v.quantize_mx, T.wq[:], T.wsc[:], T.wt[:])
-    ej = V([rn, z6, vj], v.tensor_copy, T.ej[:].indirect(T.rkn[:]), T.vj[:])
+    eg = V([em, f7], v.tensor_scalar, T.eg[0:32, :], T.em[0:32, :], -1.0, T.pf[0:32, 1:2], ALU.add, ALU.mult)
     es = V([vs, z7], v.tensor_copy, T.es[:].indirect(T.rkn[:]), T.vs[:])
-    tj = V([ej], v.transpose, T.tj[:], T.ej[:, 0:MX])
-    ts = V([es], v.transpose, T.ts[:], T.es[:, 0:MX])
-    V([tj], v.tensor_tensor, T.ex[:, 0:8], T.tj[:, 0:MX:32], T.tj[:, 16:MX:32], ALU.add)
-    ex = V([ts], v.tensor_tensor, T.ex[:, 8:16], T.ts[:, 0:MX:32], T.ts[:, 16:MX:32], ALU.add)
-    for a in range(4):
-        evx = D("y", [ex], "evx", T.er[0:32, 16 * a:16 * a + 16], T.ex[32 * a:32 * a + 32, :])
+    for q in range(8):
+        evx = D("y", [es], "evx", T.er[16:32, 16 * q:16 * q + 16], T.es[16 * q:16 * q + 1, 0:MX])
 
     tt = V([hop], v.transpose, T.tt[:], T.it[:])
     off = V([tt, pm], v.tensor_copy, T.off[:], T.tt[:].indirect(T.pm[:]))
 
-    mm = []
+    mm, have = [], [off, own, carr] + kl
     for i in range(NP):
         a, b, o = PW * i, PW * i + PW, T.off[:, PW // 16 * i:PW // 16 * (i + 1)]
-        t = V([off, k0, k1, own, carr], v.tensor_copy, T.aftq[:, a:b].bitcast(u32), T.winq[:].bitcast(u32).indirect(o))
-        pl = S([off, k0, k1, own, carr], T.afts[:, a:b], T.wins[:].indirect(o), ACT.Copy)
-        mm.append(P([t, pl, wq, sc[1]], T.py[:, 512 * i:512 * i + PW], T.wq[:], T.wsc[:], T.aftq[:, a:b], T.afts[:, a:b], True, True))
+        t = V(have, v.tensor_copy, T.aftq[:, a:b].bitcast(u32), T.winq[:].bitcast(u32).indirect(o))
+        pl = S(have, T.afts[:, a:b], T.wins[:].indirect(o), ACT.Copy)
+        mm.append(P([t, pl, wq] + [sc[k] for k in range(8)], T.py[:, 512 * i:512 * i + PW], T.wq[:], T.wsc[:], T.aftq[:, a:b], T.afts[:, a:b], True, True))
         D("y", [t], "sto", T.oc[:, 4 * a:4 * b], T.aftq[:, a:b].bitcast(u8))
 
     def y_out(i, on_v):
@@ -268,24 +284,18 @@ def rank_program(g, core, T, topo):
         D("y", [t], "sto", T.y[:, PW * i:PW * i + PW], o)
 
     y_out(0, True)
-    kk1 = V([c_kk], v.tensor_scalar, T.kk1[0:16, :], T.kk0[0:16, :], MX - 1, None, ALU.bitwise_and)
     y_out(1, True)
     y_out(2, False)
-    e0 = V([evx], v.tensor_tensor, T.e0[0:32, :], T.er[0:32, 0:32], T.er[0:32, 32:64], ALU.add)
-    z5 = V([], v.memset, T.e1[0:32, :], 0.0)
-    y_out(3, True)
+    y_out(3, False)
     for k in range(4):
-        D("s", [pl], "sto", T.osc[4 * k:4 * k + 4, :], T.afts[32 * k:32 * k + 4, :])
+        D("y", [pl], "sto", T.osc[4 * k:4 * k + 4, :], T.afts[32 * k:32 * k + 4, :])
 
-    e1 = V([e0, z5], v.tensor_tensor, T.e1[0:32, 0:16], T.e0[0:32, 0:16], T.e0[0:32, 16:32], ALU.add)
-    kk = V([kk1], v.tensor_copy, T.kk[0:16, :], T.kk1[0:16, :])
-    f7 = V([c_p], v.tensor_scalar, T.pf[:, 6:7], T.pi[:, 0:1], 8, None, ALU.is_lt)
-    e2 = V([e1], v.transpose, T.e2[0:32, :], T.e1[0:32, :])
-    em = V([kk, incl], v.tensor_scalar, T.em[0:16, :], T.kk[0:16, :], T.incl[0:16, NR * CAP - 1:NR * CAP], None, ALU.is_lt)
-    e3 = V([e2, em], v.tensor_tensor, T.e3[0:16, :], T.e2[0:16, :], T.em[0:16, :], ALU.mult)
-    eg = V([em, f7], v.tensor_scalar, T.eg[0:16, :], T.em[0:16, :], -1.0, T.pf[0:16, 6:7], ALU.add, ALU.mult)
-    e4 = V([e3, eg], v.tensor_tensor, T.e4[0:16, :], T.e3[0:16, :], T.eg[0:16, :], ALU.add)
-    D("s", [e4], "sto", T.ev[:], T.e4[0:16, :])
+    e0 = V([evx], v.tensor_tensor, T.e0[0:32, :], T.er[0:32, 0:64], T.er[0:32, 64:128], ALU.add)
+    e1 = V([e0], v.tensor_tensor, T.e1[0:32, :], T.e0[0:32, 0:32], T.e0[0:32, 32:64], ALU.add)
+    e2 = V([e1], v.tensor_tensor, T.e2[0:32, :], T.e1[0:32, 0:16], T.e1[0:32, 16:32], ALU.add)
+    e3 = V([e2], v.tensor_tensor, T.e3[0:32, :], T.e2[0:32, :], T.em[0:32, :], ALU.mult)
+    e4 = V([e3, eg], v.tensor_tensor, T.e4[0:32, :], T.e3[0:32, :], T.eg[0:32, :], ALU.add)
+    D("s", [e4], "sto", T.ev[:], T.e4[0:32, :])
 
     for name in SEMAPHORES:
         if name in total:

from concourse.bass import DstId, RemoteDMATransfer
from concourse.mybir import dt, AluOpType as ALU, ActivationFunctionType as ACT

NR, NT, NC, CAP, MX = 4, 512, 1024, 96, 256
NW = NC + NR * CAP
LC = CAP // 16
BLK = [3, 7, 2, 6, 1, 5, 0, 4]
NS = 3
VP, SP = [[4, 6], [3, 5, 7]], [[0, 2], [1]]
WD = NC + 128
TINY = 2.0 ** -120
NP, PW = 4, 256
UC = 14

SCRATCH = {"psv": ("psum", [128, 1024], "float32"), "pss": ("psum", [128, 1024], "float32"), "py": ("psum", [128, 2048], "float32")}
_SPEC = {
    "float8_e4m3fn_x4": "uq 144 urq 128 xq 512 wq 128 sndq 384 winq 1408 aftq 1024",
    "uint8": "us 144 urs 128 xs 512 wsc 128 snds 384 wins 1408 afts 1024",
    "int32": "sn8 24 ll 24 pi 8 pa 2 vo0 8 kk0 16 kk1 16",
    "uint16": "su 24 lu 24 ul 8 rkd 16 rkn 8 off 64 vo 8 pm 4",
    "bfloat16": "u0 16 ua 576 xt 2048 wt 512 eq 1024 eqm 384 w01 528 fl 384 incl 384 csg 768 cm3 1152 cm4 1152 cm5 1152 cm6 1152 cm7 1152 sg0 1024 sg1 1024 sg2 1024",
    "float16": "co 192 scn 4608",
    "float32": "df0 1024 df1 1024 df2 1024 scol 8 acc1 4 acc2 4 base 4 csum 2 ksl 2 kfl 2 a2 64 b2 64 "
               "pos 264 pt 256 it 64 tt 64 ysb 1024 pf 2 kcol 2 kcoh 2 js 256 vj 128 vs 128 pm0 4 kk 16 "
               "sr 1024 ej 1024 es 1024 er 128 e0 64 e1 32 e2 16 e3 16 e4 16 em 16 eg 16",
}
for _d in _SPEC:
    _w = _SPEC[_d].split()
    for _i in range(0, len(_w), 2):
        SCRATCH[_w[_i]] = ("sbuf", [128, int(_w[_i + 1])], _d)
SEMAPHORES = "qv qs qt qg lsn lu0 lk0 lk1 lk2 lx lw lown own hop evx sto larr carr sent".split()


def rank_program(g, core, T, topo):
    me = T.rank_of(core)
    if me is None:
        return
    seen, total = {}, {}
    v, queues = g.vector, {"v": g.vector, "s": g.scalar, "t": g.tensor, "g": g, "y": g.sync}
    u8, u32, FL = dt.uint8, dt.uint32, {"allow_small_or_imprecise_dtypes": True}

    def wait(q, deps):
        for name, val in deps:
            if seen.get((q, name), 0) < val:
                queues[q].wait_ge(T.sem[name], val)
                seen[(q, name)] = val

    def tick(name, n):
        total[name] = total.get(name, 0) + n
        return (name, total[name])

    def V(deps, f, *a):
        wait("v", deps); f(*a).then_inc(T.sem.qv, 1); return tick("qv", 1)

    def S(deps, out, in_, func, **k):
        wait("s", deps); g.scalar.activation(out, in_, func, **k).then_inc(T.sem.qs, 1); return tick("qs", 1)

    def P(deps, *a):
        wait("t", deps); g.tensor.matmul_mx(*a).then_inc(T.sem.qt, 1); return tick("qt", 1)

    def G(deps, f, *a, **k):
        wait("g", list(deps) + [("qg", total.get("qg", 0))]); f(*a, **k).then_inc(T.sem.qg, 1); return tick("qg", 1)

    def D(q, deps, sem, out, in_):
        wait(q, deps); queues[q].dma_start(out, in_).then_inc(T.sem[sem], 16); return tick(sem, 16)

    kl = []
    for i, (a, b) in enumerate(((0, 256), (256, 512), (512, 1024))):
        D("y", [], "lk%d" % i, T.winq[:, a:b].bitcast(u8), T.kc[:, 4 * a:4 * b])
        kl.append(D("y", [], "lk%d" % i, T.wins[:, a:b], T.ks[:, a:b]))
    u0 = D("s", [], "lu0", T.u0[:], T.u[:, 0:16])
    for q in range(8):
        sn = D("s" if q < 6 else "y", [], "lsn", T.sn8[16 * q:16 * q + 16, :], T.sn[:])
    xl = D("y", [], "lx", T.xt[:], T.x[:])
    wl = D("y", [], "lw", T.wt[:], T.w[:])

    G([], g.iota, T.pi[:, 0:4], [[0, 4]], 0, 1)
    c_p = G([], g.iota, T.pi[:, 4:8], [[0, 4]], 0, 4)
    c_pm = G([], g.iota, T.pm0[:], [[32, 2], [-2, 2]], 3, 0, **FL)
    c_kk = G([], g.iota, T.kk0[0:32, :], [[1, 16]], 0, 16)
    for a in range(4):
        c_k = G([], g.iota, T.kcol[32 * a:32 * a + 32, :], [[32, 2]], 64 * a, 1, **FL)
    c_vo = G([], g.iota, T.vo0[:], [[-128, 4], [512, 2]], 384, 1)
    for b in range(4):
        c_js = G([], g.iota, T.js[:, 64 * b:64 * b + 64], [[512, 2], [0, 2], [1, 16]], 384 - 128 * b, 1, **FL)
    c_vj = G([], g.iota, T.vj[:], [[-128, 4], [512, 2], [1, 16]], 384, 1, **FL)

    others = [d for d in range(NR) if d != me]
    emask = {d: sum(1 << e for e in topo.engines(core, T.cores[d])[2 * i:2 * i + 2]) for i, d in enumerate(others)}

    def send(deps, sem, src, dst):
        wait("g", deps)
        tr = []
        for d in others:
            rid, pid = topo.addr(T.cores[d])[0:2]
            tr.append(RemoteDMATransfer(dst_ids=[DstId(rid=rid, pnc=pid)], dma_engine_mask=emask[d], remote_sem=T.sem[sem],
                                        src=src(d), dst=dst(d)))
        g.remote_dma_fused(tr, local_sem=T.sem.sent)
        tick("sent", 2 * len(others))

    send([sn], "larr", lambda d: T.sn8[:, LC * d:LC * d + LC], lambda d: T.ll[:, LC * me:LC * me + LC])
    larr = tick("larr", 2 * len(others))
    lown = D("y", [sn], "lown", T.ll[:, LC * me:LC * me + LC], T.sn8[:, LC * me:LC * me + LC])

    z_u = V([], v.memset, T.ua[:], 0.0)
    z_l = V([], v.memset, T.ul[:], UC)
    t = V([u0, z_u], v.tensor_copy, T.ua[:, 4 * UC:4 * UC + 4], T.u0[:, 0:4])
    uq = V([t], v.quantize_mx, T.uq[:], T.us[:], T.ua[:])
    ur = V([uq, z_l], v.tensor_copy, T.urq[:].bitcast(u32), T.uq[:].bitcast(u32).indirect(T.ul[:]))
    S([z_u], T.w01[:, 1:513], T.ua[:, 64:576], ACT.Identity, bias=1.0, scale=0.0)
    us = S([uq, z_l], T.urs[:], T.us[:].indirect(T.ul[:]), ACT.Copy)
    z2 = S([], T.w01[:, 0:1], T.ua[:, 64:65], ACT.Copy)
    z3 = S([], T.a2[:], T.ua[:, 64:128], ACT.Copy)
    z8 = S([], T.pos[:, MX:MX + 8], T.ua[:, 64:72], ACT.Copy)
    V([c_p], v.tensor_scalar, T.pa[:, 0:1], T.pi[:, 4:5], 28, None, ALU.bitwise_and)
    a2 = V([], v.tensor_scalar, T.pa[:, 1:2], T.pi[:, 0:1], 3, 1, ALU.logical_shift_right, ALU.bitwise_and)
    f7 = V([], v.tensor_scalar, T.pf[:, 1:2], T.pi[:, 0:1], 16, None, ALU.is_lt)
    f6 = V([a2], v.tensor_tensor, T.pf[:, 0:1], T.pa[:, 0:1], T.pa[:, 1:2], ALU.subtract)
    kk1 = V([c_kk], v.tensor_scalar, T.kk1[0:32, :], T.kk0[0:32, :], MX - 1, None, ALU.bitwise_and)
    pm = V([f6, c_pm], v.tensor_scalar, T.pm[:], T.pm0[:], T.pf[:, 0:1], None, ALU.add)
    kk = V([kk1], v.tensor_copy, T.kk[0:32, :], T.kk1[0:32, :])
    kc = V([c_k], v.tensor_scalar, T.kcoh[:], T.kcol[:], 0.5, None, ALU.add)

    def rows(ps, h):
        a, b = 512 * h, 512 * h + 512
        return P([ur, us, kl[h + 1]], ps[:, a:b], T.urq[:], T.urs[:], T.winq[:, a:b], T.wins[:, a:b], True, True)

    sc = {}

    def cols(bank, places, dep):
        for i in places:
            b, o = 128 * BLK[i], UC - 2 * i
            sc[i] = P([uq, dep], T.py[:, 512 * bank:512 * bank + 128], T.winq[:, b:b + 128], T.wins[:, b:b + 128],
                      T.uq[:, o:o + 128], T.us[:, o:o + 128], i == places[0], i == places[-1])

    rv, rs = [], []
    cols(0, VP[0], kl[0])
    rv.append(rows(T.psv, 0))
    cols(1, SP[0], kl[1])
    rs.append(rows(T.pss, 0))
    cols(2, VP[1], kl[2])
    rv.append(rows(T.psv, 1))
    cols(3, SP[1], kl[2])
    rs.append(rows(T.pss, 1))

    def columns(h, on_v):
        places, bank = (VP if on_v else SP)[h], 512 * (2 * h + (not on_v))
        i, j = places[0], places[-1] + 1
        o, p, d = T.scol[:, i:j:2], T.py[:, bank + 2 * i:bank + 2 * j:4], [sc[places[-1]]]
        t = V(d, v.tensor_copy, o, p) if on_v else S(d, o, p, ACT.Copy)
        for k in places:
            sc[k] = t

    def s_diff(i, a, b):
        return S([rs[a // 512], rs[(b - 1) // 512], sc[i]], T["df%d" % i][:, a:b], T.pss[:, a:b], ACT.Identity, bias=T.scol[:, i:i + 1], scale=-1.0)

    def s_sign(i, d):
        b, df, sg = 128 * BLK[i], T["df%d" % i], T["sg%d" % i]
        S([d], sg[:, 0:b], df[:, 0:b], ACT.Sign, bias=TINY, accum_out=T.acc1[:, i:i + 1])
        return S([d], sg[:, b:NC], df[:, b:NC], ACT.Sign, bias=-TINY, accum_out=T.acc2[:, i:i + 1])

    def v_cmp(i, a, b):
        m, cm, t = min(max(128 * BLK[i], a), b), T["cm%d" % i], None
        for lo, hi, op in ((a, m, ALU.is_le), (m, b, ALU.is_lt)):
            if lo < hi:
                t = V([rv[lo // 512], rv[(hi - 1) // 512], sc[i]], v.tensor_scalar, cm[:, lo:hi], T.psv[:, lo:hi], T.scol[:, i:i + 1], 2.0, op, ALU.mult)
        return t

    def v_sum(i, c):
        cm, o = T["cm%d" % i], WD // 2 * i
        return V([c, eqm[i]], v.tensor_tensor_scan, T.scn[:, o:o + WD // 2], cm[:, 0:WD // 2], cm[:, WD // 2:WD], 0.0, ALU.add, ALU.add)

    def v_eq(h, places):
        for i in places:
            b = 128 * BLK[i]
            eqt[i] = V([sc[i], rv[h]], v.tensor_scalar, T.eq[:, 128 * i:128 * i + 128], T.psv[:, b:b + 128], T.scol[:, i:i + 1], 2.0, ALU.is_equal, ALU.mult)

    def g_eq(i):
        eqm[i] = G([eqt[i]], g.affine_select, T["cm%d" % i][:, NC:WD], T.eq[:, 128 * i:128 * i + 128], [[-1, 128]], ALU.is_gt, 0.0, 0, 1)

    eqt, eqm = {}, {}
    columns(0, True)
    columns(0, False)
    s_diff(0, 0, 512)
    v_eq(0, VP[0])
    s_diff(2, 0, 512)
    for i in VP[0]:
        g_eq(i)
    v_cmp(4, 0, 512)
    v_cmp(6, 0, 512)
    v_eq(0, SP[0])
    su = V([sn], v.tensor_copy, T.su[:], T.sn8[:])
    columns(1, True)
    columns(1, False)
    v_eq(1, VP[1])
    for i in VP[1]:
        g_eq(i)
    d0 = s_diff(0, 512, 1024)
    s_sign(0, d0)
    c4 = v_cmp(4, 512, 1024)
    v_eq(1, SP[1])
    eqs = G([eqt[1]], g.affine_select, T.eqm[:], T.eq[:, 0:128 * NS], [[0, NS], [-1, 128]], ALU.is_gt, 0.0, 0, 1)
    xq = V([xl], v.quantize_mx, T.xq[:], T.xs[:], T.xt[:])
    c6 = v_cmp(6, 512, 1024)
    pq = V([xq, su], v.tensor_copy, T.sndq[:].bitcast(u32), T.xq[:].bitcast(u32).indirect(T.su[:]))
    ps = S([xq, su], T.snds[:], T.xs[:].indirect(T.su[:]), ACT.Copy)
    w0, own0 = NC + CAP * me, CAP * me
    send([pq], "carr", lambda d: T.sndq[:, CAP * d:CAP * d + CAP].bitcast(u8), lambda d: T.winq[:, w0:w0 + CAP].bitcast(u8))
    send([ps], "carr", lambda d: T.snds[:, CAP * d:CAP * d + CAP], lambda d: T.wins[:, w0:w0 + CAP])
    carr = tick("carr", 4 * len(others))
    D("y", [pq], "own", T.winq[:, w0:w0 + CAP].bitcast(u8), T.sndq[:, own0:own0 + CAP].bitcast(u8))
    own = D("y", [ps], "own", T.wins[:, w0:w0 + CAP], T.snds[:, own0:own0 + CAP])
    z6 = G([], g.iota, T.ej[:, 0:MX], [[0, MX]], 0, 0, **FL)
    z7 = G([], g.iota, T.es[:, 0:MX], [[0, MX]], 0, 0, **FL)

    v_sum(4, c4)
    d2 = s_diff(2, 512, 1024)
    lu = V([larr, lown], v.tensor_scalar, T.lu[:], T.ll[:], 1.0, None, ALU.add)
    fl = S([lu, z2], T.fl[:], T.w01[:].indirect(T.lu[:]), ACT.Copy)
    s_sign(2, d2)
    c3 = v_cmp(3, 0, 1024)
    v_sum(6, c6)
    incl = V([fl], v.tensor_tensor_scan, T.incl[:], T.fl[:], T.fl[:], 0.0, ALU.add, ALU.max)
    for h in range(2):
        cs = S([incl, kc], T.csg[:, 384 * h:384 * h + 384], T.incl[:], ACT.Sign, bias=T.kcoh[:, h:h + 1], scale=-1.0, accum_out=T.csum[:, h:h + 1])
    d1 = s_diff(1, 0, 1024)
    c5 = v_cmp(5, 0, 1024)
    sg = s_sign(1, d1)
    v_sum(3, c3)
    co, n64 = {}, float(NC)
    for i in range(NS):
        a = 128 * i
        co[i] = V([eqs], v.tensor_tensor_scan, T.co[:, 64 * i:64 * i + 64], T.eqm[:, a:a + 64], T.eqm[:, a + 64:a + 128], n64, ALU.add, ALU.add)
        if i == 0:
            sl = V([cs], v.tensor_scalar, T.ksl[:], T.csum[:], 0.5, float(NC + NR * CAP // 2), ALU.mult, ALU.add)
        if i == 1:
            kf = V([sl], v.tensor_scalar, T.kfl[:], T.ksl[:], float(NW), None, ALU.is_lt)
    km = V([kf, z3], v.tensor_tensor, T.a2[:, 0:64:32], T.ksl[:], T.kfl[:], ALU.mult)
    v_sum(5, c5)
    b2 = V([km], v.transpose, T.b2[:], T.a2[:])
    for a in range(4):
        pos = G([b2], g.partition_broadcast, T.pos[:, 64 * a:64 * a + 64], T.b2[32 * a:32 * a + 1, :], 128)
    c7 = v_cmp(7, 0, 1024)
    sm = v_sum(7, c7)
    last, step = WD // 2 - 1, WD // 2
    bs = V([sg, co[NS - 1]], v.tensor_tensor, T.base[:, 0:NS], T.co[:, 63:64 * NS:64], T.acc1[:, 0:NS], ALU.add)
    cn = V([bs], v.tensor_tensor, T.scn[:, last:NS * step:step], T.base[:, 0:NS], T.acc2[:, 0:NS], ALU.add)
    cnt = T.scn[:, last:8 * step:step]

    V([cn, sm], v.tensor_scalar, T.rkd[:, 0:16:2], cnt, 0.5, float(MX), ALU.mult, ALU.min)
    rd = V([], v.tensor_scalar, T.rkd[:, 1:16:2], cnt, 0.5, float(MX), ALU.mult, ALU.min)
    rn = V([], v.tensor_scalar, T.rkn[:], cnt, 0.5, None, ALU.mult)
    pt = V([rd, pos, z8, c_js], v.tensor_tensor, T.pt[:], T.pos[:].indirect(T.rkd[:]), T.js[:], ALU.max)
    for a in range(4):
        hop = D("y", [pt], "hop", T.it[32 * a:32 * a + 32, :], T.pt[0:128:16, :])

    vo = V([c_vo], v.tensor_copy, T.vo[:], T.vo0[:])
    sr = S([], T.sr[:], T.pss[:], ACT.Copy)
    vs = S([sr, vo], T.vs[:], T.sr[:].indirect(T.vo[:]), ACT.Copy)
    em = V([kk, incl], v.tensor_scalar, T.em[0:32, :], T.kk[0:32, :], T.incl[0:32, NR * CAP - 1:NR * CAP], None, ALU.is_lt)
    ej = V([rn, z6, c_vj], v.tensor_copy, T.ej[:].indirect(T.rkn[:]), T.vj[:])
    for q in range(8):
        D("s", [ej], "evx", T.er[0:16, 16 * q:16 * q + 16], T.ej[16 * q:16 * q + 1, 0:MX])
    wq = V([wl], v.quantize_mx, T.wq[:], T.wsc[:], T.wt[:])
    eg = V([em, f7], v.tensor_scalar, T.eg[0:32, :], T.em[0:32, :], -1.0, T.pf[0:32, 1:2], ALU.add, ALU.mult)
    es = V([vs, z7], v.tensor_copy, T.es[:].indirect(T.rkn[:]), T.vs[:])
    for q in range(8):
        evx = D("y", [es], "evx", T.er[16:32, 16 * q:16 * q + 16], T.es[16 * q:16 * q + 1, 0:MX])

    tt = V([hop], v.transpose, T.tt[:], T.it[:])
    off = V([tt, pm], v.tensor_copy, T.off[:], T.tt[:].indirect(T.pm[:]))

    mm, have = [], [off, own, carr] + kl
    for i in range(NP):
        a, b, o = PW * i, PW * i + PW, T.off[:, PW // 16 * i:PW // 16 * (i + 1)]
        t = V(have, v.tensor_copy, T.aftq[:, a:b].bitcast(u32), T.winq[:].bitcast(u32).indirect(o))
        pl = S(have, T.afts[:, a:b], T.wins[:].indirect(o), ACT.Copy)
        mm.append(P([t, pl, wq] + [sc[k] for k in range(8)], T.py[:, 512 * i:512 * i + PW], T.wq[:], T.wsc[:], T.aftq[:, a:b], T.afts[:, a:b], True, True))
        D("y", [t], "sto", T.oc[:, 4 * a:4 * b], T.aftq[:, a:b].bitcast(u8))

    def y_out(i, on_v):
        o, p = T.ysb[:, PW * i:PW * i + PW], T.py[:, 512 * i:512 * i + PW]
        t = V([mm[i]], v.tensor_copy, o, p) if on_v else S([mm[i]], o, p, ACT.Copy)
        D("y", [t], "sto", T.y[:, PW * i:PW * i + PW], o)

    y_out(0, True)
    y_out(1, True)
    y_out(2, False)
    y_out(3, False)
    for k in range(4):
        D("y", [pl], "sto", T.osc[4 * k:4 * k + 4, :], T.afts[32 * k:32 * k + 4, :])

    e0 = V([evx], v.tensor_tensor, T.e0[0:32, :], T.er[0:32, 0:64], T.er[0:32, 64:128], ALU.add)
    e1 = V([e0], v.tensor_tensor, T.e1[0:32, :], T.e0[0:32, 0:32], T.e0[0:32, 32:64], ALU.add)
    e2 = V([e1], v.tensor_tensor, T.e2[0:32, :], T.e1[0:32, 0:16], T.e1[0:32, 16:32], ALU.add)
    e3 = V([e2], v.tensor_tensor, T.e3[0:32, :], T.e2[0:32, :], T.em[0:32, :], ALU.mult)
    e4 = V([e3, eg], v.tensor_tensor, T.e4[0:32, :], T.e3[0:32, :], T.eg[0:32, :], ALU.add)
    D("s", [e4], "sto", T.ev[:], T.e4[0:32, :])

    for name in SEMAPHORES:
        if name in total:
            wait("g", [(name, total[name])])
